import numpy as np, ml_dtypes
CORES = [23,119,17,113]
N = 4
BF = ml_dtypes.bfloat16
def gentries(a):
    return np.ascontiguousarray(a.reshape(8, 16, -1).transpose(0, 2, 1)).reshape(8, -1)
def gtable(e):
    e = np.asarray(e); return np.ascontiguousarray(e.reshape(8, -1, 16).transpose(0, 2, 1)).reshape(128, -1).astype(np.int32)
S, R, B, C, P, STEPS, O = 2048, 2048, 64, 3, 2, 3, 192
def pick(t, l):
    return np.stack([np.stack([np.take(t[r, g], l[r, g], axis=1) for g in range(8)]) for r in range(N)])
def widen(t, send):
    s = pick(t, send)
    return np.stack([np.concatenate([t[r]] + [s[(r + 1 + m) % N][:, :, (N - 2 - m) * B:(N - 1 - m) * B] for m in range(N - 1)], axis=2) for r in range(N)])
def groups(a):
    return np.stack([gentries(v) for v in a])
def first(v):
    u, i, n = np.unique(v, return_index=True, return_inverse=True); return i[n.reshape(-1)]
def network(rng, pairs):
    reac = np.zeros((N, 8, 2 * R), np.int64); cons = np.full((N, 8, C * S), R + O); sp = np.zeros((N, 8, O), np.int64); rx = np.zeros((N, 8, O), np.int64)
    for g in range(8):
        inc, use = [], []
        for r in range(N):
            if pairs:
                inc.append((rng.permutation(R)[:, None] + R * np.arange(2)).reshape(-1)); use.append((rng.permutation(S)[:, None] + S * np.arange(C)).reshape(-1)[:2 * R])
            else:
                inc.append(rng.permutation(2 * R)); use.append(rng.permutation(C * S)[:2 * R])
            e, u = inc[r], use[r]
            rx[r, g] = e[:O] % R; sp[r, g] = u[:O] % S
            reac[r, g, e[O:]] = u[O:] % S; cons[r, g, u[O:]] = e[O:] % R
        for r in range(N):
            for m in range(N - 1):
                q, k = (r + 1 + m) % N, N - 2 - m
                e = inc[r][m * B:(m + 1) * B]; u = use[q][k * B:(k + 1) * B]; n = np.arange(B); j = n if pairs else rng.permutation(B)
                reac[r, g, e] = S + m * B + (first(u % S) if pairs else j)
                cons[q, g, u[j]] = R + k * B + (first(e % R) if pairs else n)
    prod = rng.integers(0, R + O, (N, 8, P * S)); prod[rng.random(prod.shape) < 0.25] = R + O
    return reac, cons, prod, sp, rx
def pack(x, rate, net):
    return dict([("x", np.ascontiguousarray(np.reshape(x, (N, 128, S))).astype(np.int32)), ("rate", rate.astype(np.int32))] + [(n, np.stack([gtable(e) for e in v])) for n, v in zip(("reac", "cons", "prod", "spsend", "rxsend"), net)])
def some(rng):
    return rng.integers(0, 256, (N, 8, 16, S)) >> rng.integers(0, 8, (N, 8, 16, S)), rng.integers(1, 128, (N, 8, R)) >> rng.integers(0, 4, (N, 8, R))
def setup_inputs(rng):
    net = network(rng, False); x, k = some(rng); return pack(x, k, net)
def setup_inputs_ties(rng):
    net = network(rng, False); n = np.sum(net[1].reshape(N, 8, C, S) != R + O, axis=2)[:, :, None]
    x = np.where(n < 2, 5 + rng.integers(0, 4, (N, 8, 16, S)), 3 * n - rng.integers(0, 2, (N, 8, 16, S)))
    return pack(x, rng.integers(123, 128, (N, 8, R)), net)
def setup_inputs_twins(rng):
    net = network(rng, True); x, k = some(rng); return pack(x, k, net)
def setup_inputs_ends(rng):
    net = network(rng, False); p = rng.choice(np.array([0, R - 1, R, R + O - 1, R + O]), (N, 8, P * S))
    x = 255 * (rng.random((N, 8, 16, S)) < 0.9); k = 127 * (rng.random((N, 8, R)) < 0.9)
    return pack(x, k, net[:2] + (p,) + net[3:])
def setup_inputs_spread(rng):
    net = network(rng, False); w = rng.random((N, 8, 1, S)); x = rng.integers(0, 256, (N, 8, 16, S))
    x = np.where(w < 0.05, 0, np.where(w < 0.15, 255, np.where(w < 0.5, x, x >> 5)))
    w = rng.random((N, 8, R)); k = rng.integers(0, 128, (N, 8, R)); k = np.where(w < 0.05, 0, np.where(w < 0.15, 127, np.where(w < 0.5, k, k >> 4)))
    return pack(x, k, net)
def check_inputs(d):
    try:
        top = {"x": 255, "rate": 127, "reac": S + O - 1, "cons": R + O, "prod": R + O, "spsend": S - 1, "rxsend": R - 1}
        bad = [n + " range" for n in top if d[n].min() < 0 or d[n].max() > top[n]]
        if bad: return bad
        ra, co, ss, rs = groups(d["reac"]), groups(d["cons"]), groups(d["spsend"]), groups(d["rxsend"])
        ids = np.broadcast_to(np.arange(N * S, dtype=np.int64).reshape(N, 1, 1, S), (N, 8, 1, S)); idr = np.broadcast_to(np.arange(N * R, dtype=np.int64).reshape(N, 1, 1, R), (N, 8, 1, R))
        net = np.arange(8, dtype=np.int64).reshape(1, 8, 1); own = np.arange(N, dtype=np.int64).reshape(N, 1, 1)
        a = (net * (N * S) + pick(widen(ids, ss), ra)[:, :, 0]) * (N * R) + own * R + np.arange(2 * R) % R
        w = pick(np.concatenate([widen(idr, rs), np.full((N, 8, 1, 1), -1)], axis=3), co)[:, :, 0]
        b = ((net * (N * S) + own * S + np.arange(C * S) % S) * (N * R) + w)[w >= 0]
        return [] if np.array_equal(np.sort(a.reshape(-1)), np.sort(b)) else ["cons fits reac"]
    except Exception:
        return ["form"]
def reference(x, rate, reac, cons, prod, spsend, rxsend):
    n = x.astype(np.int32).reshape(N, 8, 16, S); k = rate.astype(np.int32)[:, :, None]; none = np.zeros((N, 8, 16, 1), np.int32)
    ra, co, pr, ss, rs = groups(reac), groups(cons), groups(prod), groups(spsend), groups(rxsend)
    for step in range(STEPS):
        a = pick(widen(n, ss), ra)
        f = np.minimum(3, (k * a[..., :R] * a[..., R:]) >> 10)
        w = np.concatenate([widen(f, rs), none], axis=3)
        demand = np.sum(pick(w, co).reshape(N, 8, 16, C, S), axis=3)
        veto = (demand > n).astype(np.int32)
        b = pick(widen(veto, ss), ra)
        f = f * ((b[..., :R] + b[..., R:]) == 0)
        w = np.concatenate([widen(f, rs), none], axis=3)
        n = n - np.sum(pick(w, co).reshape(N, 8, 16, C, S), axis=3) + np.sum(pick(w, pr).reshape(N, 8, 16, P, S), axis=3)
    return {"y": n.reshape(N, 128, S).astype(np.float32)}

@@ -1,0 +1,462 @@
+from concourse.bass import DstId, RemoteDMATransfer
+from concourse.mybir import AluOpType, ActivationFunctionType
+
+S, O, B, STEPS = 2048, 192, 64, 3
+NONE = S + O
+WW = NONE + 8
+
+SCRATCH = {
+    "xi": ("sbuf", [128, S], "int32"),
+    "sl": ("sbuf", [128, 24], "int32"),
+    "hl": ("sbuf", [128, 48], "int32"),
+    "su": ("sbuf", [128, 24], "uint16"),
+    "hu": ("sbuf", [128, 48], "uint16"),
+    "li": ("sbuf", [128, 896], "int32"),
+    "lu": ("sbuf", [128, 896], "uint16"),
+    "cu": ("sbuf", [128, 84], "uint16"),
+    "ri": ("sbuf", [128, 512], "int32"),
+    "rb": ("sbuf", [128, 512], "bfloat16"),
+    "kk": ("sbuf", [128, S], "bfloat16"),
+    "kc": ("sbuf", [128, O], "bfloat16"),
+    "ones": ("sbuf", [128, 512], "bfloat16"),
+    "ip": ("sbuf", [128, 128], "bfloat16"),
+    "im": ("sbuf", [128, 128], "bfloat16"),
+    "ib": ("sbuf", [128, 128], "bfloat16"),
+    "jp": ("sbuf", [128, 128], "float32"),
+    "jm": ("sbuf", [128, 128], "float32"),
+    "sel": ("sbuf", [128, 512], "bfloat16"),
+    "it": ("sbuf", [128, 32], "int32"),
+    "iu": ("sbuf", [128, 32], "int32"),
+    "idb": ("sbuf", [128, 16], "bfloat16"),
+    "zz": ("sbuf", [128, 144], "float32"),
+    "mk": ("sbuf", [128, 2 * O], "bfloat16"),
+    "xx": ("sbuf", [128, 7 * O], "float32"),
+    "tb": ("sbuf", [128, S], "float32"),
+    "tc": ("sbuf", [128, O], "float32"),
+    "gb": ("sbuf", [128, 5 * O], "bfloat16"),
+    "yy": ("sbuf", [128, S], "float32"),
+}
+for _l in range(5):
+    SCRATCH["ga%d" % _l] = ("sbuf", [128, S], "bfloat16")
+for _t in range(STEPS):
+    SCRATCH["n%d" % _t] = ("sbuf", [128, NONE], "float32")
+    SCRATCH["f%d" % _t] = ("sbuf", [128, WW], "bfloat16")
+    SCRATCH["m%d" % _t] = ("sbuf", [128, NONE], "bfloat16")
+    SCRATCH["h%d" % _t] = ("sbuf", [128, WW], "bfloat16")
+    SCRATCH["nc%d" % _t] = ("sbuf", [128, O], "float32")
+    SCRATCH["fc%d" % _t] = ("sbuf", [128, O], "bfloat16")
+    SCRATCH["mc%d" % _t] = ("sbuf", [128, O], "bfloat16")
+    SCRATCH["hc%d" % _t] = ("sbuf", [128, O], "bfloat16")
+for _b in range(8):
+    SCRATCH["ps%d" % _b] = ("psum", [128, 512], "float32")
+
+SEMAPHORES = (["cv", "ca", "ct", "cp", "sent", "stored"] + ["ld%d" % _k for _k in range(8)]
+              + ["ar%d" % _k for _k in range(4 * STEPS)])
+
+SCHED = {
+    "engines": (4, 4),
+    "B1": [0, 448, 832, 1280, 1664, 1792, 2048],
+    "P1v": "tc t:0:64 vc t:64:512 t:512:2048 v:0 v:1 v:2 v:3 v:5 v:4 F:5",
+    "P1a": "x:0:384 Fc x:384:1280 x:1280:2048 F:0 F:1 F:2 F:3 F:4",
+    "B2": [0, 448, 960, 1408, 1856, 1952, 2048],
+    "P2v": "dc g2:0:576 Mc g1:0:512 g2:576:2048 M:0 M:1 M:2 M:3",
+    "P2a": "ac g1:512:1472 g0:0:1088 g0:1088:1952 g1:1472:1856 g1:1856:2048 g0:1952:2048 M:4 M:5",
+    "B3": [0, 320, 544, 832, 1344, 1760, 2048],
+    "P3v": "tc t:0:320 Ec t:320:864 t:864:1536 t:1536:2048 E:1 E:2 E:4",
+    "P3a": "mc m:0:544 m:544:832 m:832:1344 m:1344:2048 E:0 E:3 E:5",
+    "B4": [1120, 1504, 1888, 2048],
+    "P4v": "c0:0:800 c0:800:1120 c1:0:800 Nc c1:800:1120 c2:0:800 c2:800:1120 c3:0:800 c3:800:1120 c4:0:800 c4:800:1120 N:1",
+    "P4a": "ac g2:1120:2048 g4:1120:2048 g0:1120:2048 g1:1120:2048 g3:1120:1632 g3:1632:1888 g3:1888:2048 N:0 N:2",
+    "B5": [1056, 1216, 1440, 1760, 2048],
+    "P5v": "c0:0:256 c0:256:352 c1:0:96 c1:96:256 c2:0:96 c0:352:608 c3:0:96 c1:256:352 c4:0:96 c2:96:352 N:0 c3:96:352 "
+           "c1:352:608 c4:96:352 c2:352:608 N:1 c3:352:608 c0:608:1056 c4:352:608 c1:608:1056 N:2 c2:608:768 c2:768:1056 "
+           "c3:608:768 c3:768:1056 c4:608:1056",
+    "P5a": "g2:1056:1280 g0:1056:1440 g4:1056:1216 g1:1056:1216 g3:1056:1440 g1:1216:1760 g4:1216:1440 g2:1280:1760 "
+           "g4:1440:2048 g3:1440:1792 g0:1440:2048 g1:1760:2048 g2:1760:2048 g3:1792:2048 N:3",
+    "Y": [(0, 96), (1056, 1216), (96, 352), (1216, 1440), (352, 608), (1440, 1760), (1760, 2048), (608, 1056)],
+    "S0v": "ones zz0 no0 no1 no2 no3 no4 no5 ian iz idb zz1 su hi lo hu im ib xc rb cv:0:512 "
+           "X0 X1 X2 X3 X4 X5 X6 cv:512:2048 lu:0:256 lu:256:896 cu",
+}
+
+
+def rank_program(g, core, T, topo):
+    rank = T.rank_of(core)
+    if rank is None:
+        return
+    A, F = AluOpType, ActivationFunctionType
+    cores = list(T.cores)
+    N = len(cores)
+    eng = {"v": g.vector, "a": g.scalar, "t": g.tensor, "p": g, "s": g.sync}
+    ops, acc, named = [], {}, {}
+    phase = [0]
+
+    def r(name, c0=None, c1=None, step=1, parts=128):
+        if c0 is None:
+            c0, c1 = 0, SCRATCH[name][1][1]
+        return (name, c0, c1, step, parts)
+
+    def ap(x):
+        name, c0, c1, step, parts = x
+        rows = slice(0, parts) if parts < 128 else slice(None)
+        return T[name][rows, c0:c1:step] if step > 1 else T[name][rows, c0:c1]
+
+    def ind(win, off):
+        return ap(win).indirect(ap(off))
+
+    def add(q, name, emit, reads, writes, kind="c", sem=None, count=1, group=None):
+        k = len(ops)
+        deps = set()
+        for xs, wr in ((reads, False), (writes, True)):
+            for x in xs:
+                psum = SCRATCH[x[0]][0] == "psum"
+                for (c0, c1, j, w) in acc.get(x[0], []):
+                    o = ops[j]
+                    if psum:
+                        if group is not None and o["group"] == group:
+                            continue
+                        if w or wr or o["q"] != q:
+                            deps.add(j)
+                    elif (w or wr) and c0 < x[2] and x[1] < c1:
+                        deps.add(j)
+        for xs, wr in ((reads, False), (writes, True)):
+            for x in xs:
+                acc.setdefault(x[0], []).append((x[1], x[2], k, wr))
+        ops.append({"q": q, "name": name, "emit": emit, "deps": deps, "kind": kind, "sem": sem, "count": count,
+                    "group": group, "phase": phase[0], "pos": k, "rate": 1.0,
+                    "width": (writes[0][2] - writes[0][1]) // writes[0][3] if writes else 0})
+        named[(phase[0], q, name)] = k
+        return ops[k]
+
+    def order(q, text):
+        for i, name in enumerate(text.split()):
+            ops[named[(phase[0], q, name)]]["pos"] = i - 10000
+
+    V, SC, PE = g.vector, g.scalar, g.tensor
+
+    def rate(o, off):
+        o["rate"] = 1.3 if off else 1.0
+
+    def tt(name, out, in0, in1, op, off=None):
+        rate(add("v", name, lambda: V.tensor_tensor(ap(out), ind(in0, off) if off else ap(in0), ap(in1), op),
+                 [in0, in1] + ([off] if off else []), [out]), off)
+
+    def ts(name, out, in0, s1, s2, op0, op1=None, off=None):
+        def emit():
+            src = ind(in0, off) if off else ap(in0)
+            if op1 is None:
+                return V.tensor_scalar(ap(out), src, s1, None, op0)
+            return V.tensor_scalar(ap(out), src, s1, s2, op0, op1)
+        rate(add("v", name, emit, [in0] + ([off] if off else []), [out]), off)
+
+    def cp(name, out, in_, off=None):
+        rate(add("v", name, lambda: V.tensor_copy(ap(out), ind(in_, off) if off else ap(in_)),
+                 [in_] + ([off] if off else []), [out]), off)
+
+    def act(name, out, in_, func, bias=None, scale=None, off=None):
+        def emit():
+            src = ind(in_, off) if off else ap(in_)
+            if bias is None:
+                return SC.activation(ap(out), src, func)
+            return SC.activation(ap(out), src, func, bias=bias, scale=scale)
+        rate(add("a", name, emit, [in_] + ([off] if off else []), [out]), off)
+
+    groups = [0]
+
+    def mm(terms):
+        groups[0] += 1
+        whole = max(t[0][2] - t[0][1] for t in terms)
+        for i, (out, lhs, rhs) in enumerate(terms):
+            o = add("t", "mm%d_%d" % (groups[0], i), lambda out=out, lhs=lhs, rhs=rhs: (ap(out), ap(lhs), ap(rhs)),
+                    [lhs, rhs], [out], group=groups[0])
+            o["full"] = out[2] - out[1] == whole
+            o["rate"] = 2.0 if SCRATCH[rhs[0]][2] == "float32" else 0.5
+
+    loads = [0]
+
+    def load(q, out, src):
+        sem = "ld%d" % loads[0]
+        loads[0] += 1
+        add(q, sem, lambda: eng[q].dma_start(ap(out), src), [], [out], kind="d", sem=sem, count=16)
+
+    peers = [cores[(rank + 1 + m) % N] for m in range(N - 1)]
+
+    def masks_of(src):
+        used, res = [], {}
+        for d in sorted([c for c in cores if c != src], key=lambda d: len(topo.engines(src, d))):
+            want = SCHED["engines"][1 if topo.chip(src) == topo.chip(d) else 0]
+            e = [x for x in topo.engines(src, d) if x not in used][:want]
+            used += e
+            res[d] = e
+        return res
+
+    mine = masks_of(core)
+    arrive = sum(len(masks_of(c)[core]) for c in peers)
+    leave = sum(len(e) for e in mine.values())
+    sends = [0]
+
+    def exchange(src, win):
+        sem = "ar%d" % sends[0]
+        sends[0] += 1
+
+        def emit():
+            trs = []
+            for m, d in enumerate(peers):
+                rid, pid = topo.addr(d)[:2]
+                c = S + (N - 2 - m) * B
+                trs.append(RemoteDMATransfer(dst_ids=[DstId(rid=rid, pnc=pid)], dma_engine_mask=sum(1 << e for e in mine[d]),
+                                             remote_sem=T.sem[sem], src=T[src][:, m * B:(m + 1) * B], dst=T[win][:, c:c + B]))
+            return g.remote_dma_fused(trs, local_sem=T.sem.sent)
+        add("p", "send", emit, [r(src)], [], kind="r")
+        add("x", "arrive", None, [], [r(win, S, NONE)], kind="x", sem=sem, count=arrive)
+
+    def lst(l, a, b):
+        return r("lu", 128 * l + a // 16, 128 * l + b // 16)
+
+    def cl(l0, l1):
+        return r("cu", 12 * l0, 12 * l1)
+
+    def spans(text, key):
+        return [(int(w.split(":")[1]), int(w.split(":")[2])) for w in text.split() if w.split(":")[0] == key and w.count(":") == 2]
+
+    def has(text, name):
+        return name in text.split()
+
+    def banks(key):
+        bs = SCHED[key]
+        return [(k, bs[k], bs[k + 1], r("ps%d" % (k + 1), 0, bs[k + 1] - bs[k])) for k in range(len(bs) - 1)]
+
+    IP, IM, IB, JP, JM = r("ip"), r("im"), r("ib"), r("jp"), r("jm")
+    PC = r("ps0", 0, O)
+
+    load("a", r("sl", 0, 12), T.spsend[:])
+    load("s", r("xi"), T.x[:])
+    load("a", r("sl", 12, 24), T.rxsend[:])
+    load("s", r("ri", parts=32), T.rate[:])
+    load("s", r("li", 0, 256), T.reac[:])
+    load("s", r("li", 256, 640), T.cons[:])
+    load("s", r("li", 640, 896), T.prod[:])
+    add("v", "ones", lambda: V.memset(ap(r("ones")), 1.0), [], [r("ones")])
+    add("v", "zz0", lambda: V.memset(ap(r("zz")), 0.0), [], [r("zz")])
+    add("p", "i1", lambda: g.iota(ap(r("it", 0, 16)), [[-1, 16]], 16, 1), [], [r("it", 0, 16)])
+    add("p", "i2", lambda: g.iota(ap(r("it", 16, 24)), [[-16, 8]], 0, 1), [], [r("it", 16, 24)])
+    add("p", "ip", lambda: g.affine_select(ap(IP), ap(r("ones", 0, 128)), [[-1, 128]], A.is_equal, 0.0, 0, 1), [r("ones")], [IP])
+    add("p", "sel", lambda: g.affine_select(ap(r("sel", parts=32)), ap(r("ones", parts=32)), [[-1, 4], [-4, 8], [0, 16]],
+                                            A.is_equal, 0.0, 0, 1), [r("ones")], [r("sel")])
+    cp("su", r("su"), r("sl"))
+    ts("hi", r("hl", 0, 24), r("sl"), 4, None, A.arith_shift_right)
+    ts("lo", r("hl", 24, 48), r("sl"), 15, None, A.bitwise_and)
+    cp("hu", r("hu"), r("hl"))
+    ts("im", IM, IP, -1.0, None, A.mult)
+    ts("ib", IB, IP, 256.0, None, A.mult)
+    act("jp", JP, IP, F.Copy)
+    act("jm", JM, IM, F.Copy)
+    ts("ian", r("iu", 0, 16), r("it", 0, 16), 15, None, A.bitwise_and)
+    ts("iz", r("iu", 16, 24), r("it", 16, 24), 4, None, A.arith_shift_right)
+    ts("idb", r("idb"), r("iu", 0, 16), 0.0, None, A.is_equal)
+    ts("zz1", r("zz", 15, 143, 16), r("iu", 16, 24), 0.0, None, A.is_equal)
+    cp("rb", r("rb", parts=32), r("ri", parts=32))
+    for t in range(STEPS):
+        add("v", "no%d" % (2 * t), lambda t=t: V.memset(ap(r("f%d" % t, NONE, WW)), 253.0 / 256), [], [r("f%d" % t, NONE, WW)])
+        add("v", "no%d" % (2 * t + 1), lambda t=t: V.memset(ap(r("h%d" % t, NONE, WW)), 0.0), [], [r("h%d" % t, NONE, WW)])
+    act("mk", r("mk"), r("idb"), F.Copy, off=r("hu", 24, 48))
+    for u in range(4):
+        mm([(r("ps%d" % (u + 1)), r("sel", 128 * u, 128 * u + 128, parts=32), r("rb", parts=32))])
+        act("kk%d" % u, r("kk", 512 * u, 512 * u + 512), r("ps%d" % (u + 1)), F.Copy)
+    act("kc", r("kc"), r("kk"), F.Copy, off=r("su", 12, 24))
+    cp("xc", r("nc0"), r("xi"), off=r("su", 0, 12))
+    exchange("nc0", "n0")
+    for a, b in spans(SCHED["S0v"], "cv"):
+        cp("cv:%d:%d" % (a, b), r("n0", a, b), r("xi", a, b))
+    for l in range(7):
+        s = 1 if l < 2 else 0
+        tt("X%d" % l, r("xx", O * l, O * l + O), r("li", 128 * l, 128 * l + 128), r("mk", O * s, O * s + O), A.mult,
+           off=r("hu", 12 * s, 12 * s + 12))
+    mm([(r("ps7", 0, 84), r("zz", 15 - u, 143 - u), r("xx", u, 7 * O, 16)) for u in range(16)])
+    for a, b in spans(SCHED["S0v"], "lu"):
+        cp("lu:%d:%d" % (a, b), r("lu", a, b), r("li", a, b))
+    cp("cu", r("cu"), r("ps7", 0, 84))
+    order("v", SCHED["S0v"])
+
+    FS, FB = 1.0 / (1024 * 256), (252.5 + 1.0 / 2048) / 256
+    stores = [0]
+    for t in range(STEPS):
+        n, f, m, h = "n%d" % t, "f%d" % t, "m%d" % t, "h%d" % t
+        nc, fc, mc, hc = "nc%d" % t, "fc%d" % t, "mc%d" % t, "hc%d" % t
+        phase[0] += 1
+        sv, sa = SCHED["P1v"], SCHED["P1a"]
+
+        def floor(name, out, in_):
+            if has(sv, name):
+                ts(name, out, in_, FS, FB, A.mult, A.add)
+            else:
+                act(name, out, in_, F.Identity, FB, FS)
+        tt("tc", r("tc"), r(n), r("kc"), A.mult, off=cl(1, 2))
+        tt("vc", r("tc"), r(n), r("tc"), A.mult, off=cl(0, 1))
+        floor("Fc", r(fc), r("tc"))
+        exchange(fc, f)
+        for a, b in spans(sv, "t"):
+            tt("t:%d:%d" % (a, b), r("tb", a, b), r(n), r("kk", a, b), A.mult, off=lst(1, a, b))
+        for a, b in spans(sa, "x"):
+            act("x:%d:%d" % (a, b), r("ga0", a, b), r(n), F.Copy, off=lst(0, a, b))
+        for k, a, b, ps in banks("B1"):
+            mm([(ps, IP, r("ga0", a, b))])
+            tt("v:%d" % k, r("tb", a, b), r("tb", a, b), ps, A.mult)
+            floor("F:%d" % k, r(f, a, b), r("tb", a, b))
+        order("v", sv)
+        order("a", sa)
+        phase[0] += 1
+        sv, sa = SCHED["P2v"], SCHED["P2a"]
+        FW = r(f)
+
+        def mask(name, out, ps, cnt, terms):
+            if has(sv, name):
+                mm(terms)
+                tt(name, out, ps, cnt, A.is_le)
+            else:
+                mm([(ps, JM, cnt)] + terms)
+                act(name, out, ps, F.Sign, 0.5, -1.0)
+        act("ac", r("gb", 0, 2 * O), FW, F.Relu, 256.0, -256.0, off=cl(2, 4))
+        ts("dc", r("gb", 2 * O, 3 * O), FW, 1.0, 247.0 / 256, A.min, A.subtract, off=cl(4, 5))
+        mask("Mc", r(mc), PC, r(nc), [(PC, IB, r("gb", 2 * O, 3 * O)), (PC, IM, r("gb", 0, O)), (PC, IM, r("gb", O, 2 * O))])
+        exchange(mc, m)
+        parts = []
+        for l in range(3):
+            for a, b in spans(sa, "g%d" % l):
+                act("g%d:%d:%d" % (l, a, b), r("ga%d" % l, a, b), FW, F.Relu, 256.0, -256.0, off=lst(2 + l, a, b))
+                parts.append((l, a, b, IM))
+            for a, b in spans(sv, "g%d" % l):
+                ts("g%d:%d:%d" % (l, a, b), r("ga%d" % l, a, b), FW, 1.0, 247.0 / 256 if l == 2 else 1.0, A.min, A.subtract,
+                   off=lst(2 + l, a, b))
+                parts.append((l, a, b, IB))
+        for k, a, b, ps in banks("B2"):
+            mask("M:%d" % k, r(m, a, b), ps, r(n, a, b),
+                 [(r(ps[0], max(a, c) - a, min(b, d) - a), mat, r("ga%d" % l, max(a, c), min(b, d)))
+                  for (l, c, d, mat) in parts if max(a, c) < min(b, d)])
+        order("v", sv)
+        order("a", sa)
+        phase[0] += 1
+        sv, sa = SCHED["P3v"], SCHED["P3a"]
+
+        def left(name, out, ps):
+            if has(sv, name):
+                ts(name, out, ps, 509.0, 0.0, A.subtract, A.max)
+            else:
+                act(name, out, ps, F.Relu, -509.0, 1.0)
+        tt("tc", r("gb", 0, O), r(m), r(fc), A.min, off=cl(1, 2))
+        act("mc", r("gb", O, 2 * O), r(m), F.Copy, off=cl(0, 1))
+        mm([(PC, IB, r("gb", 0, O)), (PC, IB, r("gb", O, 2 * O))])
+        left("Ec", r(hc), PC)
+        exchange(hc, h)
+        for a, b in spans(sv, "t"):
+            tt("t:%d:%d" % (a, b), r("ga3", a, b), r(m), r(f, a, b), A.min, off=lst(1, a, b))
+        for a, b in spans(sa, "m"):
+            act("m:%d:%d" % (a, b), r("ga4", a, b), r(m), F.Copy, off=lst(0, a, b))
+        for k, a, b, ps in banks("B3"):
+            mm([(ps, IB, r("ga3", a, b)), (ps, IB, r("ga4", a, b))])
+            left("E:%d" % k, r(h, a, b), ps)
+        order("v", sv)
+        order("a", sa)
+        phase[0] += 1
+        last = t == STEPS - 1
+        sv, sa = SCHED["P5v" if last else "P4v"], SCHED["P5a" if last else "P4a"]
+        new = "yy" if last else "n%d" % (t + 1)
+        HW = r(h)
+
+        def counts(name, out, ps, old, terms):
+            if has(sv, name):
+                mm(terms)
+                tt(name, out, ps, old, A.add)
+            else:
+                mm([(ps, JP, old)] + terms)
+                act(name, out, ps, F.Copy)
+        if not last:
+            act("ac", r("gb"), HW, F.Copy, off=cl(2, 7))
+            counts("Nc", r("nc%d" % (t + 1)), PC, r(nc), [(PC, IM if l < 3 else IP, r("gb", O * l, O * l + O)) for l in range(5)])
+            exchange("nc%d" % (t + 1), new)
+        for l in range(5):
+            for a, b in spans(sv, "c%d" % l):
+                tt("c%d:%d:%d" % (l, a, b), r(new if l == 4 else "tb", a, b), HW, r(n if l == 0 else "tb", a, b),
+                   A.subtract if l in (0, 3) else A.add, off=lst(2 + l, a, b))
+            for a, b in spans(sa, "g%d" % l):
+                act("g%d:%d:%d" % (l, a, b), r("ga%d" % l, a, b), HW, F.Copy, off=lst(2 + l, a, b))
+        for k, a, b, ps in banks("B5" if last else "B4"):
+            counts("N:%d" % k, r(new, a, b), ps, r(n, a, b), [(ps, IM if l < 3 else IP, r("ga%d" % l, a, b)) for l in range(5)])
+        order("v", sv)
+        order("a", sa)
+        if last:
+            for i, (a, b) in enumerate(SCHED["Y"]):
+                add("s", "st%d" % i, lambda a=a, b=b: g.sync.dma_start(T.y[:, a:b], ap(r("yy", a, b))), [r("yy", a, b)], [],
+                    kind="d", sem="stored", count=16)
+                stores[0] += 16
+
+    queue, members = {}, {}
+    for k, o in enumerate(ops):
+        if o["q"] != "t":
+            queue.setdefault(o["q"], []).append(k)
+        else:
+            members[o["group"]] = members.get(o["group"], 0) + 1
+    for q in queue:
+        queue[q].sort(key=lambda k: (ops[k]["phase"], ops[k]["pos"]))
+    pend = [k for k, o in enumerate(ops) if o["q"] == "t"]
+    head = dict((q, 0) for q in queue)
+    done, free, seq, opened = {}, dict((q, 0.0) for q in "vatpsx"), [], {}
+    while len(seq) < len(ops):
+        cand = [queue[q][head[q]] for q in queue if head[q] < len(queue[q])]
+        first = min([ops[k]["phase"] for k in pend] + [99])
+        cand += [k for k in pend if ops[k]["phase"] == first and (ops[k]["full"] or ops[k]["group"] in opened)]
+        cand = [k for k in cand if all(d in done for d in ops[k]["deps"])]
+        assert cand, "the queues' orders contradict the data's order"
+        best = min(cand, key=lambda k: (max([free[ops[k]["q"]]] + [done[d] for d in ops[k]["deps"]]), k))
+        o = ops[best]
+        start = max([free[o["q"]]] + [done[d] for d in o["deps"]])
+        cost = (0 if o["q"] == "t" else 55) + max(64, o["width"]) * o["rate"] if o["kind"] == "c" else 0.0
+        free[o["q"]] = start + cost
+        done[best] = start + cost + (3000 if o["kind"] == "d" else 120)
+        if o["q"] == "t":
+            pend.remove(best)
+            o["start"] = o["group"] not in opened
+            opened[o["group"]] = opened.get(o["group"], 0) + 1
+            o["stop"] = opened[o["group"]] == members[o["group"]]
+        else:
+            head[o["q"]] += 1
+        seq.append(best)
+
+    count = dict((q, 0) for q in "vatp")
+    known = dict((q, {}) for q in "vatps")
+    clock, token, waited = {}, {}, {}
+    place = dict((k, i) for i, k in enumerate(seq))
+    for k in seq:
+        o = ops[k]
+        q = o["q"]
+        if o["kind"] == "x":
+            token[k] = (o["sem"], o["count"])
+            clock[k] = {o["sem"]: o["count"]}
+            continue
+        kn = known[q]
+        for d in sorted(o["deps"], key=lambda d: -place[d]):
+            sem, val = token[d]
+            if kn.get(sem, 0) >= val:
+                continue
+            eng[q].wait_ge(T.sem[sem], val)
+            waited[sem] = max(waited.get(sem, 0), val)
+            for s2, v2 in clock[d].items():
+                if kn.get(s2, 0) < v2:
+                    kn[s2] = v2
+        ins = o["emit"]()
+        if q == "t":
+            ins = PE.matmul(ins[0], ins[1], ins[2], o["start"], o["stop"])
+        if o["kind"] == "c":
+            count[q] += 1
+            token[k] = ("c" + q, count[q])
+            ins.then_inc(T.sem["c" + q], 1)
+        elif o["kind"] == "d":
+            token[k] = (o["sem"], o["count"])
+            ins.then_inc(T.sem[o["sem"]], 16)
+        if o["kind"] != "r":
+            clock[k] = dict(kn)
+            clock[k][token[k][0]] = token[k][1]
+    for q in "vatp":
+        if waited.get("c" + q, 0) < count[q]:
+            g.wait_ge(T.sem["c" + q], count[q])
+    g.wait_ge(T.sem.sent, leave * sends[0])
+    g.sync.wait_ge(T.sem.stored, stores[0])

@@ -2,8 +2,28 @@ from concourse.bass import DstId, RemoteDMATransfer
 from concourse.mybir import AluOpType, ActivationFunctionType
 
 S, O, B, STEPS = 2048, 192, 64, 3
-NONE = S + O
-WW = NONE + 8
+U = O + S
+NONE = U + O
+WW = NONE + 16
+L = U // 16
+
+SCHED = {
+    "engines": (4, 4),
+    "xparts": 4,
+    "ahead": ((1, 1, 1, 2), (2, 2, 4)),
+    "akh": True,
+    "acv": True,
+    "P1v": "t:0:192 t:192:512 s:0:192 t:512:960 F:0:192 u:192:512 k:960:2240 u:512:960 s:960:1920 s:1920:2240 F:1120:1920 F:1920:2240",
+    "P1a": "x:0:192 y:960:2240 x:960:1920 x:1920:2240 F:192:960 F:960:1120",
+    "P2v": "P C:192:704:1184 e:0:192@2",
+    "P2a": "G:0:192 G:1184:1600:2048:2240",
+    "P3v": "C:0:192 C:192:736:1280",
+    "P3a": "G:1280:1696:2112:2240",
+    "P4v": "C:192:768:1376 e:0:192@3",
+    "P4a": "G:0:192 G:1376:1792:2112:2240",
+    "P5v": "C:192:480:768 C:768:928:1088 C:1088:1184:1280",
+    "P5a": "G:1280:1568:1856:2112:2240",
+}
 
 SCRATCH = {
     "xi": ("sbuf", [128, S], "int32"),
@@ -11,17 +31,17 @@ SCRATCH = {
     "hl": ("sbuf", [128, 48], "int32"),
     "su": ("sbuf", [128, 24], "uint16"),
     "hu": ("sbuf", [128, 48], "uint16"),
-    "li": ("sbuf", [128, 896], "int32"),
-    "lu": ("sbuf", [128, 896], "uint16"),
-    "cu": ("sbuf", [128, 84], "uint16"),
+    "li": ("sbuf", [128, 7, 128], "int32"),
+    "lu": ("sbuf", [128, 7, L], "uint16"),
+    "la": ("sbuf", [128, 1280], "uint16"),
     "ri": ("sbuf", [128, 512], "int32"),
     "rb": ("sbuf", [128, 512], "bfloat16"),
-    "kk": ("sbuf", [128, S], "bfloat16"),
-    "kc": ("sbuf", [128, O], "bfloat16"),
+    "kk": ("sbuf", [128, U], "float32"),
+    "kh": ("sbuf", [128, U], "float16"),
     "ones": ("sbuf", [128, 512], "bfloat16"),
     "ip": ("sbuf", [128, 128], "bfloat16"),
     "im": ("sbuf", [128, 128], "bfloat16"),
-    "ib": ("sbuf", [128, 128], "bfloat16"),
+    "iq": ("sbuf", [128, 128], "bfloat16"),
     "jp": ("sbuf", [128, 128], "float32"),
     "jm": ("sbuf", [128, 128], "float32"),
     "sel": ("sbuf", [128, 512], "bfloat16"),
@@ -31,52 +51,27 @@ SCRATCH = {
     "zz": ("sbuf", [128, 144], "float32"),
     "mk": ("sbuf", [128, 2 * O], "bfloat16"),
     "xx": ("sbuf", [128, 7 * O], "float32"),
-    "tb": ("sbuf", [128, S], "float32"),
-    "tc": ("sbuf", [128, O], "float32"),
-    "gb": ("sbuf", [128, 5 * O], "bfloat16"),
-    "yy": ("sbuf", [128, S], "float32"),
+    "x1": ("sbuf", [128, U], "bfloat16"),
+    "x2": ("sbuf", [128, U], "bfloat16"),
+    "kx": ("sbuf", [128, U], "float16"),
+    "zh": ("sbuf", [128, U], "float16"),
+    "tb": ("sbuf", [128, U], "bfloat16"),
+    "tf": ("sbuf", [128, U], "float32"),
+    "yy": ("sbuf", [128, U], "float32"),
 }
-for _l in range(5):
-    SCRATCH["ga%d" % _l] = ("sbuf", [128, S], "bfloat16")
+for _l in range(4):
+    SCRATCH["ga%d" % _l] = ("sbuf", [128, 5 * 512], "bfloat16")
 for _t in range(STEPS):
     SCRATCH["n%d" % _t] = ("sbuf", [128, NONE], "float32")
+    SCRATCH["e%d" % _t] = ("sbuf", [128, WW], "bfloat16")
     SCRATCH["f%d" % _t] = ("sbuf", [128, WW], "bfloat16")
     SCRATCH["m%d" % _t] = ("sbuf", [128, NONE], "bfloat16")
     SCRATCH["h%d" % _t] = ("sbuf", [128, WW], "bfloat16")
-    SCRATCH["nc%d" % _t] = ("sbuf", [128, O], "float32")
-    SCRATCH["fc%d" % _t] = ("sbuf", [128, O], "bfloat16")
-    SCRATCH["mc%d" % _t] = ("sbuf", [128, O], "bfloat16")
-    SCRATCH["hc%d" % _t] = ("sbuf", [128, O], "bfloat16")
 for _b in range(8):
     SCRATCH["ps%d" % _b] = ("psum", [128, 512], "float32")
 
-SEMAPHORES = (["cv", "ca", "ct", "cp", "sent", "stored"] + ["ld%d" % _k for _k in range(8)]
+SEMAPHORES = (["cv", "ca", "ct", "cp", "sent", "stored"] + ["ld%d" % _k for _k in range(12)]
               + ["ar%d" % _k for _k in range(4 * STEPS)])
-
-SCHED = {
-    "engines": (4, 4),
-    "B1": [0, 448, 832, 1280, 1664, 1792, 2048],
-    "P1v": "tc t:0:64 vc t:64:512 t:512:2048 v:0 v:1 v:2 v:3 v:5 v:4 F:5",
-    "P1a": "x:0:384 Fc x:384:1280 x:1280:2048 F:0 F:1 F:2 F:3 F:4",
-    "B2": [0, 448, 960, 1408, 1856, 1952, 2048],
-    "P2v": "dc g2:0:576 Mc g1:0:512 g2:576:2048 M:0 M:1 M:2 M:3",
-    "P2a": "ac g1:512:1472 g0:0:1088 g0:1088:1952 g1:1472:1856 g1:1856:2048 g0:1952:2048 M:4 M:5",
-    "B3": [0, 320, 544, 832, 1344, 1760, 2048],
-    "P3v": "tc t:0:320 Ec t:320:864 t:864:1536 t:1536:2048 E:1 E:2 E:4",
-    "P3a": "mc m:0:544 m:544:832 m:832:1344 m:1344:2048 E:0 E:3 E:5",
-    "B4": [1120, 1504, 1888, 2048],
-    "P4v": "c0:0:800 c0:800:1120 c1:0:800 Nc c1:800:1120 c2:0:800 c2:800:1120 c3:0:800 c3:800:1120 c4:0:800 c4:800:1120 N:1",
-    "P4a": "ac g2:1120:2048 g4:1120:2048 g0:1120:2048 g1:1120:2048 g3:1120:1632 g3:1632:1888 g3:1888:2048 N:0 N:2",
-    "B5": [1056, 1216, 1440, 1760, 2048],
-    "P5v": "c0:0:256 c0:256:352 c1:0:96 c1:96:256 c2:0:96 c0:352:608 c3:0:96 c1:256:352 c4:0:96 c2:96:352 N:0 c3:96:352 "
-           "c1:352:608 c4:96:352 c2:352:608 N:1 c3:352:608 c0:608:1056 c4:352:608 c1:608:1056 N:2 c2:608:768 c2:768:1056 "
-           "c3:608:768 c3:768:1056 c4:608:1056",
-    "P5a": "g2:1056:1280 g0:1056:1440 g4:1056:1216 g1:1056:1216 g3:1056:1440 g1:1216:1760 g4:1216:1440 g2:1280:1760 "
-           "g4:1440:2048 g3:1440:1792 g0:1440:2048 g1:1760:2048 g2:1760:2048 g3:1792:2048 N:3",
-    "Y": [(0, 96), (1056, 1216), (96, 352), (1216, 1440), (352, 608), (1440, 1760), (1760, 2048), (608, 1056)],
-    "S0v": "ones zz0 no0 no1 no2 no3 no4 no5 ian iz idb zz1 su hi lo hu im ib xc rb cv:0:512 "
-           "X0 X1 X2 X3 X4 X5 X6 cv:512:2048 lu:0:256 lu:256:896 cu",
-}
 
 
 def rank_program(g, core, T, topo):
@@ -97,6 +92,9 @@ def rank_program(g, core, T, topo):
 
     def ap(x):
         name, c0, c1, step, parts = x
+        if len(SCRATCH[name][1]) == 3:
+            w = SCRATCH[name][1][2]
+            return T[name][:, c0 // w, c0 % w:c0 % w + c1 - c0]
         rows = slice(0, parts) if parts < 128 else slice(None)
         return T[name][rows, c0:c1:step] if step > 1 else T[name][rows, c0:c1]
 
@@ -122,61 +120,59 @@ def rank_program(g, core, T, topo):
             for x in xs:
                 acc.setdefault(x[0], []).append((x[1], x[2], k, wr))
         ops.append({"q": q, "name": name, "emit": emit, "deps": deps, "kind": kind, "sem": sem, "count": count,
-                    "group": group, "phase": phase[0], "pos": k, "rate": 1.0,
-                    "width": (writes[0][2] - writes[0][1]) // writes[0][3] if writes else 0})
+                    "group": group, "phase": phase[0], "pos": k})
         named[(phase[0], q, name)] = k
         return ops[k]
 
-    def order(q, text):
-        for i, name in enumerate(text.split()):
+    def order(q, names):
+        for i, name in enumerate(names):
             ops[named[(phase[0], q, name)]]["pos"] = i - 10000
 
     V, SC, PE = g.vector, g.scalar, g.tensor
 
-    def rate(o, off):
-        o["rate"] = 1.3 if off else 1.0
-
     def tt(name, out, in0, in1, op, off=None):
-        rate(add("v", name, lambda: V.tensor_tensor(ap(out), ind(in0, off) if off else ap(in0), ap(in1), op),
-                 [in0, in1] + ([off] if off else []), [out]), off)
+        add("v", name, lambda: V.tensor_tensor(ap(out), ind(in0, off) if off else ap(in0), ap(in1), op),
+            [in0, in1] + ([off] if off else []), [out])
 
-    def ts(name, out, in0, s1, s2, op0, op1=None, off=None):
+    def ts(name, out, in0, s1, s2, op0, op1=None):
         def emit():
-            src = ind(in0, off) if off else ap(in0)
             if op1 is None:
-                return V.tensor_scalar(ap(out), src, s1, None, op0)
-            return V.tensor_scalar(ap(out), src, s1, s2, op0, op1)
-        rate(add("v", name, emit, [in0] + ([off] if off else []), [out]), off)
+                return V.tensor_scalar(ap(out), ap(in0), s1, None, op0)
+            return V.tensor_scalar(ap(out), ap(in0), s1, s2, op0, op1)
+        add("v", name, emit, [in0], [out])
+
+    def times(name, out, in0, in1):
+        add("v", name, lambda: V.tensor_tensor_scan(ap(out), ap(in0), ap(in1), 0.0, A.max, A.mult), [in0, in1], [out])
 
     def cp(name, out, in_, off=None):
-        rate(add("v", name, lambda: V.tensor_copy(ap(out), ind(in_, off) if off else ap(in_)),
-                 [in_] + ([off] if off else []), [out]), off)
+        add("v", name, lambda: V.tensor_copy(ap(out), ind(in_, off) if off else ap(in_)), [in_] + ([off] if off else []), [out])
 
     def act(name, out, in_, func, bias=None, scale=None, off=None):
         def emit():
             src = ind(in_, off) if off else ap(in_)
-            if bias is None:
+            if scale is None:
                 return SC.activation(ap(out), src, func)
+            if bias is None:
+                return SC.activation(ap(out), src, func, scale=scale)
             return SC.activation(ap(out), src, func, bias=bias, scale=scale)
-        rate(add("a", name, emit, [in_] + ([off] if off else []), [out]), off)
+        add("a", name, emit, [in_] + ([off] if off else []), [out])
 
-    groups = [0]
+    groups, members, opened = [0], {}, {}
 
-    def mm(terms):
-        groups[0] += 1
-        whole = max(t[0][2] - t[0][1] for t in terms)
-        for i, (out, lhs, rhs) in enumerate(terms):
-            o = add("t", "mm%d_%d" % (groups[0], i), lambda out=out, lhs=lhs, rhs=rhs: (ap(out), ap(lhs), ap(rhs)),
-                    [lhs, rhs], [out], group=groups[0])
-            o["full"] = out[2] - out[1] == whole
-            o["rate"] = 2.0 if SCRATCH[rhs[0]][2] == "float32" else 0.5
+    def mm(terms, group=None):
+        if group is None:
+            groups[0] += 1
+            group = groups[0]
+        for (out, lhs, rhs) in terms:
+            add("t", "mm%d" % len(ops), lambda out=out, lhs=lhs, rhs=rhs: (ap(out), ap(lhs), ap(rhs)), [lhs, rhs], [out], group=group)
+        return group
 
     loads = [0]
 
-    def load(q, out, src):
+    def load(q, outs, dst, src):
         sem = "ld%d" % loads[0]
         loads[0] += 1
-        add(q, sem, lambda: eng[q].dma_start(ap(out), src), [], [out], kind="d", sem=sem, count=16)
+        add(q, sem, lambda: eng[q].dma_start(dst, src), [], outs, kind="d", sem=sem, count=16)
 
     peers = [cores[(rank + 1 + m) % N] for m in range(N - 1)]
 
@@ -194,7 +190,7 @@ def rank_program(g, core, T, topo):
     leave = sum(len(e) for e in mine.values())
     sends = [0]
 
-    def exchange(src, win):
+    def exchange(buf):
         sem = "ar%d" % sends[0]
         sends[0] += 1
 
@@ -202,229 +198,260 @@ def rank_program(g, core, T, topo):
             trs = []
             for m, d in enumerate(peers):
                 rid, pid = topo.addr(d)[:2]
-                c = S + (N - 2 - m) * B
+                c = U + (N - 2 - m) * B
                 trs.append(RemoteDMATransfer(dst_ids=[DstId(rid=rid, pnc=pid)], dma_engine_mask=sum(1 << e for e in mine[d]),
-                                             remote_sem=T.sem[sem], src=T[src][:, m * B:(m + 1) * B], dst=T[win][:, c:c + B]))
+                                             remote_sem=T.sem[sem], src=T[buf][:, m * B:(m + 1) * B], dst=T[buf][:, c:c + B]))
             return g.remote_dma_fused(trs, local_sem=T.sem.sent)
-        add("p", "send", emit, [r(src)], [], kind="r")
-        add("x", "arrive", None, [], [r(win, S, NONE)], kind="x", sem=sem, count=arrive)
+        add("p", "send", emit, [r(buf, 0, O)], [], kind="r")
+        add("x", "arrive", None, [], [r(buf, U, NONE)], kind="x", sem=sem, count=arrive)
+
+    def win(buf):
+        return r(buf, O, SCRATCH[buf][1][1])
 
     def lst(l, a, b):
-        return r("lu", 128 * l + a // 16, 128 * l + b // 16)
+        return r("lu", L * l + a // 16, L * l + b // 16)
 
-    def cl(l0, l1):
-        return r("cu", 12 * l0, 12 * l1)
+    def spans(bs):
+        return [(bs[k], bs[k + 1]) for k in range(len(bs) - 1) if bs[k] < bs[k + 1]]
 
-    def spans(text, key):
-        return [(int(w.split(":")[1]), int(w.split(":")[2])) for w in text.split() if w.split(":")[0] == key and w.count(":") == 2]
+    def calls(key, name):
+        return [tuple(int(v) for v in w.split(":")[1:]) for w in SCHED[key].split() if w.split(":")[0] == name]
 
-    def has(text, name):
-        return name in text.split()
+    IP, IM, IQ, JP, JM = r("ip"), r("im"), r("iq"), r("jp"), r("jm")
+    LISTS = {"P2": (2, 5), "P3": (0, 2), "P4": (2, 7), "P5": (2, 7)}
+    BANKS = {"P2": 0, "P3": 0, "P4": 4, "P5": 4}
 
-    def banks(key):
-        bs = SCHED[key]
-        return [(k, bs[k], bs[k + 1], r("ps%d" % (k + 1), 0, bs[k + 1] - bs[k])) for k in range(len(bs) - 1)]
+    def pieces(key):
+        ab = [x for bs in calls(key + "a", "G") for x in spans(bs)]
+        return [(a, b, r("ps%d" % (BANKS[key] + k), 0, b - a), "ga%d" % k) for k, (a, b) in enumerate(ab)]
 
-    IP, IM, IB, JP, JM = r("ip"), r("im"), r("ib"), r("jp"), r("jm")
-    PC = r("ps0", 0, O)
+    def chains(key):
+        return [x for bs in calls(key + "v", "C") for x in spans(bs)]
 
-    load("a", r("sl", 0, 12), T.spsend[:])
-    load("s", r("xi"), T.x[:])
-    load("a", r("sl", 12, 24), T.rxsend[:])
-    load("s", r("ri", parts=32), T.rate[:])
-    load("s", r("li", 0, 256), T.reac[:])
-    load("s", r("li", 256, 640), T.cons[:])
-    load("s", r("li", 640, 896), T.prod[:])
+    def orders(key, chain):
+        names, late = [], []
+        for w in SCHED[key + "v"].split():
+            if w[0] == "C":
+                cs = spans([int(v) for v in w.split(":")[1:]])
+                names += ["%s:%d:%d" % (c, a, b) for c in chain for a, b in cs]
+            elif "@" in w:
+                late.append(w.split("@"))
+            else:
+                names.append(w)
+        for w, i in late:
+            names.insert(int(i), w)
+        order("v", names)
+        acts, due = [], []
+        for a, b, ps, ga in pieces(key):
+            acts += ["g:%d:%d" % (a, b)] + due
+            due = [] if "e:%d:%d" % (a, b) in names else ["e:%d:%d" % (a, b)]
+        order("a", acts + due)
+
+    def on_vector(key, a, b):
+        return "e:%d:%d" % (a, b) in [w.split("@")[0] for w in SCHED[key + "v"].split()]
+
+    xs = spans([S * i // SCHED["xparts"] for i in range(SCHED["xparts"] + 1)])
+    load("a", [r("sl", 0, 12)], T.sl[:, 0:12], T.spsend[:])
+    load("a", [r("sl", 12, 24)], T.sl[:, 12:24], T.rxsend[:])
+    load("s", [r("ri")], T.ri[0:32, :], T.rate[:])
+    for a, b in xs:
+        load("s", [r("xi", a, b)], T.xi[:, a:b], T.x[:, a:b])
+    load("s", [r("li", 0, 256)], T.li[:, 0:2, :], T.reac[:])
+    load("s", [r("li", 256, 640)], T.li[:, 2:5, :], T.cons[:])
+    load("s", [r("li", 640, 896)], T.li[:, 5:7, :], T.prod[:])
     add("v", "ones", lambda: V.memset(ap(r("ones")), 1.0), [], [r("ones")])
     add("v", "zz0", lambda: V.memset(ap(r("zz")), 0.0), [], [r("zz")])
+    for t in range(STEPS):
+        for w, c in (("e", 253.0), ("h", 0.0)):
+            add("v", "no", lambda x=r("%s%d" % (w, t), NONE, WW), c=c: V.memset(ap(x), c), [], [r("%s%d" % (w, t), NONE, WW)])
     add("p", "i1", lambda: g.iota(ap(r("it", 0, 16)), [[-1, 16]], 16, 1), [], [r("it", 0, 16)])
     add("p", "i2", lambda: g.iota(ap(r("it", 16, 24)), [[-16, 8]], 0, 1), [], [r("it", 16, 24)])
     add("p", "ip", lambda: g.affine_select(ap(IP), ap(r("ones", 0, 128)), [[-1, 128]], A.is_equal, 0.0, 0, 1), [r("ones")], [IP])
     add("p", "sel", lambda: g.affine_select(ap(r("sel", parts=32)), ap(r("ones", parts=32)), [[-1, 4], [-4, 8], [0, 16]],
                                             A.is_equal, 0.0, 0, 1), [r("ones")], [r("sel")])
-    cp("su", r("su"), r("sl"))
-    ts("hi", r("hl", 0, 24), r("sl"), 4, None, A.arith_shift_right)
-    ts("lo", r("hl", 24, 48), r("sl"), 15, None, A.bitwise_and)
-    cp("hu", r("hu"), r("hl"))
-    ts("im", IM, IP, -1.0, None, A.mult)
-    ts("ib", IB, IP, 256.0, None, A.mult)
-    act("jp", JP, IP, F.Copy)
-    act("jm", JM, IM, F.Copy)
     ts("ian", r("iu", 0, 16), r("it", 0, 16), 15, None, A.bitwise_and)
     ts("iz", r("iu", 16, 24), r("it", 16, 24), 4, None, A.arith_shift_right)
+    ts("im", IM, IP, -1.0, None, A.mult)
     ts("idb", r("idb"), r("iu", 0, 16), 0.0, None, A.is_equal)
     ts("zz1", r("zz", 15, 143, 16), r("iu", 16, 24), 0.0, None, A.is_equal)
+    ts("iq", IQ, IP, -4.0, None, A.mult)
+    act("jp", JP, IP, F.Copy)
+    act("jm", JM, IM, F.Copy)
+    ts("hi", r("hl", 0, 24), r("sl"), 4, None, A.arith_shift_right)
+    ts("lo", r("hl", 24, 48), r("sl"), 15, None, A.bitwise_and)
+    cp("su", r("su"), r("sl"))
+    cp("hu", r("hu"), r("hl"))
     cp("rb", r("rb", parts=32), r("ri", parts=32))
-    for t in range(STEPS):
-        add("v", "no%d" % (2 * t), lambda t=t: V.memset(ap(r("f%d" % t, NONE, WW)), 253.0 / 256), [], [r("f%d" % t, NONE, WW)])
-        add("v", "no%d" % (2 * t + 1), lambda t=t: V.memset(ap(r("h%d" % t, NONE, WW)), 0.0), [], [r("h%d" % t, NONE, WW)])
-    act("mk", r("mk"), r("idb"), F.Copy, off=r("hu", 24, 48))
-    for u in range(4):
-        mm([(r("ps%d" % (u + 1)), r("sel", 128 * u, 128 * u + 128, parts=32), r("rb", parts=32))])
-        act("kk%d" % u, r("kk", 512 * u, 512 * u + 512), r("ps%d" % (u + 1)), F.Copy)
-    act("kc", r("kc"), r("kk"), F.Copy, off=r("su", 12, 24))
-    cp("xc", r("nc0"), r("xi"), off=r("su", 0, 12))
-    exchange("nc0", "n0")
-    for a, b in spans(SCHED["S0v"], "cv"):
-        cp("cv:%d:%d" % (a, b), r("n0", a, b), r("xi", a, b))
-    for l in range(7):
-        s = 1 if l < 2 else 0
-        tt("X%d" % l, r("xx", O * l, O * l + O), r("li", 128 * l, 128 * l + 128), r("mk", O * s, O * s + O), A.mult,
-           off=r("hu", 12 * s, 12 * s + 12))
-    mm([(r("ps7", 0, 84), r("zz", 15 - u, 143 - u), r("xx", u, 7 * O, 16)) for u in range(16)])
-    for a, b in spans(SCHED["S0v"], "lu"):
-        cp("lu:%d:%d" % (a, b), r("lu", a, b), r("li", a, b))
-    cp("cu", r("cu"), r("ps7", 0, 84))
-    order("v", SCHED["S0v"])
+    act("mk1", r("mk", O, 2 * O), r("idb"), F.Copy, off=r("hu", 36, 48))
+    act("mk0", r("mk", 0, O), r("idb"), F.Copy, off=r("hu", 24, 36))
 
-    FS, FB = 1.0 / (1024 * 256), (252.5 + 1.0 / 2048) / 256
+    def compose(l0, l1, bank):
+        s = 1 if l0 < 2 else 0
+        for l in range(l0, l1):
+            tt("X", r("xx", O * l, O * l + O), r("li", 128 * l, 128 * l + 128), r("mk", O * s, O * s + O), A.mult,
+               off=r("hu", 12 * s, 12 * s + 12))
+        mm([(r(bank, 0, 12 * (l1 - l0)), r("zz", 15 - u, 143 - u), r("xx", O * l0 + u, O * l1, 16)) for u in range(16)])
+
+    def narrow(l0, l1, end):
+        add("v", "lu", lambda: V.tensor_copy(T.lu[:, l0:l1, 12:end // 16], T.li[:, l0:l1, 0:(end - O) // 16]),
+            [r("li", 128 * l0, 128 * l1)], [lst(l, O, end) for l in range(l0, l1)])
+
+    offs, fill = {}, [60]
+
+    def piece_lists(key):
+        l0, l1 = LISTS[key]
+        for a, b, ps, ga in pieces(key):
+            if a < O:
+                offs[(l0, l1, a, b)] = r("la", 0, 12 * (l1 - l0))
+            elif (l0, l1, a, b) not in offs:
+                out = r("la", fill[0], fill[0] + (b - a) // 16 * (l1 - l0))
+                offs[(l0, l1, a, b)] = out
+                fill[0] = out[2]
+                add("v", "la", lambda out=out, a=a, b=b: V.tensor_copy(ap(out), T.li[:, l0:l1, (a - O) // 16:(b - O) // 16]),
+                    [r("li", 128 * l0, 128 * l1)], [out])
+
+    for u in (3, 2, 1, 0):
+        mm([(r("ps%d" % (u + 1)), r("sel", 128 * u, 128 * u + 128, parts=32), r("rb", parts=32))])
+        act("kk", r("kk", O + 512 * u, O + 512 * u + 512), r("ps%d" % (u + 1)), F.Copy, scale=-1.25 / 1024)
+    act("kc", r("kk", 0, O), win("kk"), F.Copy, off=r("su", 12, 24))
+    kh = min(a for a, b in calls("P1v", "k"))
+    for a, b in xs[:2]:
+        cp("cv", r("n0", O + a, O + b), r("xi", a, b))
+    cp("xc", r("n0", 0, O), r("xi"), off=r("su", 0, 12))
+    exchange("n0")
+    compose(0, 2, "ps0")
+    if SCHED["akh"]:
+        act("kh", r("kh", kh, U), r("kk", kh, U), F.Copy)
+    else:
+        cp("kh", r("kh", kh, U), r("kk", kh, U))
+    for a, b in xs[2:]:
+        if SCHED["acv"]:
+            act("cv", r("n0", O + a, O + b), r("xi", a, b), F.Copy)
+        else:
+            cp("cv", r("n0", O + a, O + b), r("xi", a, b))
+    compose(2, 7, "ps7")
+    narrow(0, 2, U)
+    add("v", "cu", lambda: V.tensor_copy(T.lu[:, 0:2, 0:12], T.ps0[:, 0:24]), [r("ps0")], [lst(0, 0, O), lst(1, 0, O)])
+    narrow(2, 7, max(b for key in ("P2", "P4", "P5") for a, b in chains(key)))
+    for key in LISTS:
+        piece_lists(key)
+
+    def part(buf, l, w):
+        return r(buf, l * w, l * w + w)
+
     stores = [0]
     for t in range(STEPS):
-        n, f, m, h = "n%d" % t, "f%d" % t, "m%d" % t, "h%d" % t
-        nc, fc, mc, hc = "nc%d" % t, "fc%d" % t, "mc%d" % t, "hc%d" % t
-        phase[0] += 1
-        sv, sa = SCHED["P1v"], SCHED["P1a"]
-
-        def floor(name, out, in_):
-            if has(sv, name):
-                ts(name, out, in_, FS, FB, A.mult, A.add)
-            else:
-                act(name, out, in_, F.Identity, FB, FS)
-        tt("tc", r("tc"), r(n), r("kc"), A.mult, off=cl(1, 2))
-        tt("vc", r("tc"), r(n), r("tc"), A.mult, off=cl(0, 1))
-        floor("Fc", r(fc), r("tc"))
-        exchange(fc, f)
-        for a, b in spans(sv, "t"):
-            tt("t:%d:%d" % (a, b), r("tb", a, b), r(n), r("kk", a, b), A.mult, off=lst(1, a, b))
-        for a, b in spans(sa, "x"):
-            act("x:%d:%d" % (a, b), r("ga0", a, b), r(n), F.Copy, off=lst(0, a, b))
-        for k, a, b, ps in banks("B1"):
-            mm([(ps, IP, r("ga0", a, b))])
-            tt("v:%d" % k, r("tb", a, b), r("tb", a, b), ps, A.mult)
-            floor("F:%d" % k, r(f, a, b), r("tb", a, b))
-        order("v", sv)
-        order("a", sa)
-        phase[0] += 1
-        sv, sa = SCHED["P2v"], SCHED["P2a"]
-        FW = r(f)
-
-        def mask(name, out, ps, cnt, terms):
-            if has(sv, name):
-                mm(terms)
-                tt(name, out, ps, cnt, A.is_le)
-            else:
-                mm([(ps, JM, cnt)] + terms)
-                act(name, out, ps, F.Sign, 0.5, -1.0)
-        act("ac", r("gb", 0, 2 * O), FW, F.Relu, 256.0, -256.0, off=cl(2, 4))
-        ts("dc", r("gb", 2 * O, 3 * O), FW, 1.0, 247.0 / 256, A.min, A.subtract, off=cl(4, 5))
-        mask("Mc", r(mc), PC, r(nc), [(PC, IB, r("gb", 2 * O, 3 * O)), (PC, IM, r("gb", 0, O)), (PC, IM, r("gb", O, 2 * O))])
-        exchange(mc, m)
-        parts = []
-        for l in range(3):
-            for a, b in spans(sa, "g%d" % l):
-                act("g%d:%d:%d" % (l, a, b), r("ga%d" % l, a, b), FW, F.Relu, 256.0, -256.0, off=lst(2 + l, a, b))
-                parts.append((l, a, b, IM))
-            for a, b in spans(sv, "g%d" % l):
-                ts("g%d:%d:%d" % (l, a, b), r("ga%d" % l, a, b), FW, 1.0, 247.0 / 256 if l == 2 else 1.0, A.min, A.subtract,
-                   off=lst(2 + l, a, b))
-                parts.append((l, a, b, IB))
-        for k, a, b, ps in banks("B2"):
-            mask("M:%d" % k, r(m, a, b), ps, r(n, a, b),
-                 [(r(ps[0], max(a, c) - a, min(b, d) - a), mat, r("ga%d" % l, max(a, c), min(b, d)))
-                  for (l, c, d, mat) in parts if max(a, c) < min(b, d)])
-        order("v", sv)
-        order("a", sa)
-        phase[0] += 1
-        sv, sa = SCHED["P3v"], SCHED["P3a"]
-
-        def left(name, out, ps):
-            if has(sv, name):
-                ts(name, out, ps, 509.0, 0.0, A.subtract, A.max)
-            else:
-                act(name, out, ps, F.Relu, -509.0, 1.0)
-        tt("tc", r("gb", 0, O), r(m), r(fc), A.min, off=cl(1, 2))
-        act("mc", r("gb", O, 2 * O), r(m), F.Copy, off=cl(0, 1))
-        mm([(PC, IB, r("gb", 0, O)), (PC, IB, r("gb", O, 2 * O))])
-        left("Ec", r(hc), PC)
-        exchange(hc, h)
-        for a, b in spans(sv, "t"):
-            tt("t:%d:%d" % (a, b), r("ga3", a, b), r(m), r(f, a, b), A.min, off=lst(1, a, b))
-        for a, b in spans(sa, "m"):
-            act("m:%d:%d" % (a, b), r("ga4", a, b), r(m), F.Copy, off=lst(0, a, b))
-        for k, a, b, ps in banks("B3"):
-            mm([(ps, IB, r("ga3", a, b)), (ps, IB, r("ga4", a, b))])
-            left("E:%d" % k, r(h, a, b), ps)
-        order("v", sv)
-        order("a", sa)
-        phase[0] += 1
+        n, e, f, m, h = "n%d" % t, "e%d" % t, "f%d" % t, "m%d" % t, "h%d" % t
         last = t == STEPS - 1
-        sv, sa = SCHED["P5v" if last else "P4v"], SCHED["P5a" if last else "P4a"]
-        new = "yy" if last else "n%d" % (t + 1)
-        HW = r(h)
+        k4 = "P5" if last else "P4"
+        phase[0] += 1
+        g2 = [mm([(ps, JM, r(n, a, b))]) for a, b, ps, ga in pieces("P2")]
+        for a, b in calls("P1a", "x"):
+            act("x:%d:%d" % (a, b), r("x1", a, b), win(n), F.Copy, off=lst(0, a, b))
+        for a, b in calls("P1a", "y"):
+            act("y:%d:%d" % (a, b), r("x2", a, b), win(n), F.Copy, off=lst(1, a, b))
+        both = [c for a, b in calls("P1v", "u") for c in range(a, b)]
+        for a, b in calls("P1v", "t"):
+            tt("t:%d:%d" % (a, b), r("tf" if a in both else "kx", a, b), win(n), r("kk", a, b), A.mult, off=lst(1, a, b))
+        for a, b in calls("P1v", "u"):
+            tt("u:%d:%d" % (a, b), r("tf", a, b), win(n), r("tf", a, b), A.mult, off=lst(0, a, b))
+        for a, b in calls("P1v", "k"):
+            times("k:%d:%d" % (a, b), r("kx", a, b), r("x2", a, b), r("kh", a, b))
+        for a, b in calls("P1v", "s"):
+            times("s:%d:%d" % (a, b), r("zh", a, b), r("x1", a, b), r("kx", a, b))
+        for a, b in calls("P1a", "F"):
+            act("F:%d:%d" % (a, b), r(e, a, b), r("tf" if a in both else "zh", a, b), F.Identity, 252.5 + 0.4 / 1024, -0.8)
+        for a, b in calls("P1v", "F"):
+            ts("F:%d:%d" % (a, b), r(e, a, b), r("tf" if a in both else "zh", a, b), -0.8, 252.5 + 0.4 / 1024, A.mult, A.add)
+        exchange(e)
+        names = SCHED["P1v"].split()
+        if t == 0:
+            cp("cu", r("la", 0, 60), r("ps7", 0, 60))
+            names.insert(names.index("F:0:192") + 1, "cu")
+        order("v", names)
+        order("a", SCHED["P1a"].split())
+        phase[0] += 1
+        ts("P", r(f), r(e), 256.0, 253.0, A.min, A.subtract)
+        for a, b in chains("P2"):
+            for l in range(3):
+                tt("c%d:%d:%d" % (l, a, b), r("tb", a, b), win(f), r("tb" if l else n, a, b), A.add if l else A.subtract,
+                   off=lst(2 + l, a, b))
+            ts("M:%d:%d" % (a, b), r(m, a, b), r("tb", a, b), 0.0, 4.0, A.is_le, A.mult)
+        g4 = []
 
-        def counts(name, out, ps, old, terms):
-            if has(sv, name):
-                mm(terms)
-                tt(name, out, ps, old, A.add)
+        def counts_ahead(upto):
+            for a4, b4, ps4, ga4 in pieces(k4)[len(g4):upto]:
+                g4.append(mm([(ps4, JP, r(n, a4, b4))]))
+        for i, (a, b, ps, ga) in enumerate(pieces("P2")):
+            act("g:%d:%d" % (a, b), r(ga, 0, 3 * (b - a)), win(e), F.Relu, 256.0, -1.0, off=offs[LISTS["P2"] + (a, b)])
+            mm([(ps, IM, part(ga, l, b - a)) for l in range(3)], g2[i])
+            if on_vector("P2", a, b):
+                ts("e:%d:%d" % (a, b), r(m, a, b), ps, -9.0, 4.0, A.is_le, A.mult)
             else:
-                mm([(ps, JP, old)] + terms)
-                act(name, out, ps, F.Copy)
-        if not last:
-            act("ac", r("gb"), HW, F.Copy, off=cl(2, 7))
-            counts("Nc", r("nc%d" % (t + 1)), PC, r(nc), [(PC, IM if l < 3 else IP, r("gb", O * l, O * l + O)) for l in range(5)])
-            exchange("nc%d" % (t + 1), new)
-        for l in range(5):
-            for a, b in spans(sv, "c%d" % l):
-                tt("c%d:%d:%d" % (l, a, b), r(new if l == 4 else "tb", a, b), HW, r(n if l == 0 else "tb", a, b),
+                act("e:%d:%d" % (a, b), r(m, a, b), ps, F.Relu, -32.0, -4.0)
+            counts_ahead(SCHED["ahead"][0][i])
+        exchange(m)
+        orders("P2", ["c0", "c1", "c2", "M"])
+        phase[0] += 1
+        for a, b in chains("P3"):
+            tt("c0:%d:%d" % (a, b), r("tb", a, b), win(m), r(f, a, b), A.min, off=lst(0, a, b))
+            tt("c1:%d:%d" % (a, b), r(h, a, b), win(m), r("tb", a, b), A.min, off=lst(1, a, b))
+        g3 = [mm([(ps, IP, r(f, a, b))]) for a, b, ps, ga in pieces("P3")]
+        for i, (a, b, ps, ga) in enumerate(pieces("P3")):
+            act("g:%d:%d" % (a, b), r(ga, 0, 2 * (b - a)), win(m), F.Relu, 1.0, -1.0, off=offs[LISTS["P3"] + (a, b)])
+            mm([(ps, IQ, part(ga, l, b - a)) for l in range(2)], g3[i])
+            if on_vector("P3", a, b):
+                ts("e:%d:%d" % (a, b), r(h, a, b), ps, 0.0, None, A.max)
+            else:
+                act("e:%d:%d" % (a, b), r(h, a, b), ps, F.Relu)
+            counts_ahead(SCHED["ahead"][1][i])
+        exchange(h)
+        orders("P3", ["c0", "c1"])
+        phase[0] += 1
+        new = "yy" if last else "n%d" % (t + 1)
+        for a, b in chains(k4):
+            for l in range(5):
+                tt("c%d:%d:%d" % (l, a, b), r(new if l == 4 else "tf", a, b), win(h), r(n if l == 0 else "tf", a, b),
                    A.subtract if l in (0, 3) else A.add, off=lst(2 + l, a, b))
-            for a, b in spans(sa, "g%d" % l):
-                act("g%d:%d:%d" % (l, a, b), r("ga%d" % l, a, b), HW, F.Copy, off=lst(2 + l, a, b))
-        for k, a, b, ps in banks("B5" if last else "B4"):
-            counts("N:%d" % k, r(new, a, b), ps, r(n, a, b), [(ps, IM if l < 3 else IP, r("ga%d" % l, a, b)) for l in range(5)])
-        order("v", sv)
-        order("a", sa)
+        for i, (a, b, ps, ga) in enumerate(pieces(k4)):
+            act("g:%d:%d" % (a, b), r(ga, 0, 5 * (b - a)), win(h), F.Copy, off=offs[LISTS[k4] + (a, b)])
+            mm([(ps, IM if l < 3 else IP, part(ga, l, b - a)) for l in range(5)], g4[i])
+            if on_vector(k4, a, b):
+                cp("e:%d:%d" % (a, b), r(new, a, b), ps)
+            else:
+                act("e:%d:%d" % (a, b), r(new, a, b), ps, F.Copy)
+        if not last:
+            exchange(new)
+        orders(k4, ["c0", "c1", "c2", "c3", "c4"])
         if last:
-            for i, (a, b) in enumerate(SCHED["Y"]):
-                add("s", "st%d" % i, lambda a=a, b=b: g.sync.dma_start(T.y[:, a:b], ap(r("yy", a, b))), [r("yy", a, b)], [],
+            ys = []
+            for done in ([(bs[0], bs[-1]) for bs in calls("P5v", "C")], [(a, b) for a, b, ps, ga in pieces("P5")]):
+                ys += [((b - done[0][0]) / (done[-1][1] - done[0][0]), a, b) for a, b in done]
+            for i, (share, a, b) in enumerate(sorted(ys)):
+                add("s", "st%d" % i, lambda a=a, b=b: g.sync.dma_start(T.y[:, a - O:b - O], ap(r("yy", a, b))), [r("yy", a, b)], [],
                     kind="d", sem="stored", count=16)
                 stores[0] += 16
 
-    queue, members = {}, {}
+    queue = {}
     for k, o in enumerate(ops):
-        if o["q"] != "t":
-            queue.setdefault(o["q"], []).append(k)
-        else:
-            members[o["group"]] = members.get(o["group"], 0) + 1
+        queue.setdefault(o["q"], []).append(k)
+        members[o["group"]] = members.get(o["group"], 0) + 1
     for q in queue:
         queue[q].sort(key=lambda k: (ops[k]["phase"], ops[k]["pos"]))
-    pend = [k for k, o in enumerate(ops) if o["q"] == "t"]
     head = dict((q, 0) for q in queue)
-    done, free, seq, opened = {}, dict((q, 0.0) for q in "vatpsx"), [], {}
+    seq, place = [], {}
     while len(seq) < len(ops):
         cand = [queue[q][head[q]] for q in queue if head[q] < len(queue[q])]
-        first = min([ops[k]["phase"] for k in pend] + [99])
-        cand += [k for k in pend if ops[k]["phase"] == first and (ops[k]["full"] or ops[k]["group"] in opened)]
-        cand = [k for k in cand if all(d in done for d in ops[k]["deps"])]
+        cand = [k for k in cand if all(d in place for d in ops[k]["deps"])]
         assert cand, "the queues' orders contradict the data's order"
-        best = min(cand, key=lambda k: (max([free[ops[k]["q"]]] + [done[d] for d in ops[k]["deps"]]), k))
-        o = ops[best]
-        start = max([free[o["q"]]] + [done[d] for d in o["deps"]])
-        cost = (0 if o["q"] == "t" else 55) + max(64, o["width"]) * o["rate"] if o["kind"] == "c" else 0.0
-        free[o["q"]] = start + cost
-        done[best] = start + cost + (3000 if o["kind"] == "d" else 120)
-        if o["q"] == "t":
-            pend.remove(best)
-            o["start"] = o["group"] not in opened
-            opened[o["group"]] = opened.get(o["group"], 0) + 1
-            o["stop"] = opened[o["group"]] == members[o["group"]]
-        else:
-            head[o["q"]] += 1
-        seq.append(best)
+        k = min(cand)
+        head[ops[k]["q"]] += 1
+        place[k] = len(seq)
+        seq.append(k)
 
     count = dict((q, 0) for q in "vatp")
     known = dict((q, {}) for q in "vatps")
     clock, token, waited = {}, {}, {}
-    place = dict((k, i) for i, k in enumerate(seq))
     for k in seq:
         o = ops[k]
         q = o["q"]
@@ -444,7 +471,8 @@ def rank_program(g, core, T, topo):
                     kn[s2] = v2
         ins = o["emit"]()
         if q == "t":
-            ins = PE.matmul(ins[0], ins[1], ins[2], o["start"], o["stop"])
+            opened[o["group"]] = opened.get(o["group"], 0) + 1
+            ins = PE.matmul(ins[0], ins[1], ins[2], opened[o["group"]] == 1, opened[o["group"]] == members[o["group"]])
         if o["kind"] == "c":
             count[q] += 1
             token[k] = ("c" + q, count[q])

@@ -6,32 +6,37 @@ U = O + S
 NONE = U + O
 WW = NONE + 16
 L = U // 16
+KS = -(1.0 - 1.8e-4) / 1536
+MID = 1120.0
 
 SCHED = {
     "engines": (4, 4),
-    "xparts": 4,
-    "ahead": ((1, 1, 1, 2), (2, 2, 4)),
-    "akh": True,
-    "acv": True,
-    "P1v": "t:0:192 t:192:512 s:0:192 t:512:960 F:0:192 u:192:512 k:960:2240 u:512:960 s:960:1920 s:1920:2240 F:1120:1920 F:1920:2240",
-    "P1a": "x:0:192 y:960:2240 x:960:1920 x:1920:2240 F:192:960 F:960:1120",
-    "P2v": "P C:192:704:1184 e:0:192@2",
-    "P2a": "G:0:192 G:1184:1600:2048:2240",
-    "P3v": "C:0:192 C:192:736:1280",
-    "P3a": "G:1280:1696:2112:2240",
-    "P4v": "C:192:768:1376 e:0:192@3",
-    "P4a": "G:0:192 G:1376:1792:2112:2240",
-    "P5v": "C:192:480:768 C:768:928:1088 C:1088:1184:1280",
-    "P5a": "G:1280:1568:1856:2112:2240",
+    "xparts": 1,
+    "last rates": "v",
+    "counts": {"P2": (0, 0, 0, 1), "P4": (0, 4, 5, 0), "P5": (4, 0, 0, 5)},
+    "P1v": "t:0:192 t:192:384 s:0:192 t:384:576 F:0:192 t:576:1568 f:0:192 s:192:1152 k:1568:2240 F:192:1152 s:1152:1600 "
+           "s:1600:2016 F:1152:1600 s:2016:2240 F:1600:2016 F:2016:2240",
+    "P1a": "x:0:192 x:192:1152 y:1568:2240 x:1152:1600 x:1600:2016 x:2016:2240 f:192:640",
+    "P2v": "f:640:896 C:192:768:1344 e:0:192@3",
+    "P2a": "g:0:192 g:1344:1808 g:1808:2080 g:2080:2240 e:1344:1808 e:1808:2080 e:2080:2240 f:896:1024",
+    "P3v": "c0:0:192 f:1024:1280 c1:0:192 C:192:736:1280",
+    "P3a": "g:1280:1696 g:1696:2048 g:2048:2240 e:1280:1696 e:1696:2048 e:2048:2240",
+    "P4v": "C:192:768:1360 e:0:192@3",
+    "P4a": "g:0:192 g:1360:1808 g:1808:2080 g:2080:2240 e:1360:1808 e:1808:2080 e:2080:2240",
+    "P5v": "c0:192:608 c0:608:1024 c1:192:608 c1:608:1024 c2:192:608 c2:608:1024 c3:192:608 c0:1024:1296 c4:192:608 "
+           "c1:1024:1296 c3:608:1024 c2:1024:1296 c4:608:1024 c3:1024:1296 e:2080:2240 c4:1024:1296",
+    "P5a": "g:1360:1808 g:1808:2080 e:1360:1808 g:2080:2240 e:1808:2080 g:1296:1360 e:1296:1360",
+    "stores": "y:1360:1808 y:192:608 y:1808:2080 y:608:1024 y:2080:2240 y:1024:1360",
 }
 
 SCRATCH = {
-    "xi": ("sbuf", [128, S], "int32"),
+    "nb": ("sbuf", [128, U], "bfloat16"),
     "sl": ("sbuf", [128, 24], "int32"),
     "hl": ("sbuf", [128, 48], "int32"),
     "su": ("sbuf", [128, 24], "uint16"),
     "hu": ("sbuf", [128, 48], "uint16"),
     "li": ("sbuf", [128, 7, 128], "int32"),
+    "lc": ("sbuf", [128, 2, 128], "float32"),
     "lu": ("sbuf", [128, 7, L], "uint16"),
     "la": ("sbuf", [128, 1280], "uint16"),
     "ri": ("sbuf", [128, 512], "int32"),
@@ -43,28 +48,29 @@ SCRATCH = {
     "im": ("sbuf", [128, 128], "bfloat16"),
     "iq": ("sbuf", [128, 128], "bfloat16"),
     "jp": ("sbuf", [128, 128], "float32"),
-    "jm": ("sbuf", [128, 128], "float32"),
     "sel": ("sbuf", [128, 512], "bfloat16"),
     "it": ("sbuf", [128, 32], "int32"),
     "iu": ("sbuf", [128, 32], "int32"),
     "idb": ("sbuf", [128, 16], "bfloat16"),
-    "zz": ("sbuf", [128, 144], "float32"),
+    "zz": ("sbuf", [128, 144], "bfloat16"),
     "mk": ("sbuf", [128, 2 * O], "bfloat16"),
-    "xx": ("sbuf", [128, 7 * O], "float32"),
-    "x1": ("sbuf", [128, U], "bfloat16"),
-    "x2": ("sbuf", [128, U], "bfloat16"),
+    "xx": ("sbuf", [128, 2 * O], "float16"),
+    "xw": ("sbuf", [128, 5 * O], "float32"),
+    "zw": ("sbuf", [128, 144], "float32"),
+    "x1": ("sbuf", [128, U], "float16"),
+    "x2": ("sbuf", [128, U], "float16"),
     "kx": ("sbuf", [128, U], "float16"),
     "zh": ("sbuf", [128, U], "float16"),
-    "tb": ("sbuf", [128, U], "bfloat16"),
+    "tb": ("sbuf", [128, U], "float16"),
     "tf": ("sbuf", [128, U], "float32"),
+    "ff": ("sbuf", [128, U], "bfloat16"),
     "yy": ("sbuf", [128, U], "float32"),
 }
 for _l in range(4):
     SCRATCH["ga%d" % _l] = ("sbuf", [128, 5 * 512], "bfloat16")
 for _t in range(STEPS):
-    SCRATCH["n%d" % _t] = ("sbuf", [128, NONE], "float32")
+    SCRATCH["n%d" % _t] = ("sbuf", [128, NONE], "float32" if _t else "int32")
     SCRATCH["e%d" % _t] = ("sbuf", [128, WW], "bfloat16")
-    SCRATCH["f%d" % _t] = ("sbuf", [128, WW], "bfloat16")
     SCRATCH["m%d" % _t] = ("sbuf", [128, NONE], "bfloat16")
     SCRATCH["h%d" % _t] = ("sbuf", [128, WW], "bfloat16")
 for _b in range(8):
@@ -94,6 +100,8 @@ def rank_program(g, core, T, topo):
         name, c0, c1, step, parts = x
         if len(SCRATCH[name][1]) == 3:
             w = SCRATCH[name][1][2]
+            if c1 - c0 > w:
+                return T[name][:, c0 // w:c1 // w, :]
             return T[name][:, c0 // w, c0 % w:c0 % w + c1 - c0]
         rows = slice(0, parts) if parts < 128 else slice(None)
         return T[name][rows, c0:c1:step] if step > 1 else T[name][rows, c0:c1]
@@ -196,7 +204,7 @@ def rank_program(g, core, T, topo):
 
         def emit():
             trs = []
-            for m, d in enumerate(peers):
+            for m, d in sorted(enumerate(peers), key=lambda md: topo.chip(md[1]) == topo.chip(core)):
                 rid, pid = topo.addr(d)[:2]
                 c = U + (N - 2 - m) * B
                 trs.append(RemoteDMATransfer(dst_ids=[DstId(rid=rid, pnc=pid)], dma_engine_mask=sum(1 << e for e in mine[d]),
@@ -214,83 +222,75 @@ def rank_program(g, core, T, topo):
     def spans(bs):
         return [(bs[k], bs[k + 1]) for k in range(len(bs) - 1) if bs[k] < bs[k + 1]]
 
-    def calls(key, name):
-        return [tuple(int(v) for v in w.split(":")[1:]) for w in SCHED[key].split() if w.split(":")[0] == name]
+    CHAIN = {"P2": "c0 c1 c2 M", "P3": "c0 c1", "P4": "c0 c1 c2 c3 c4", "P5": "c0 c1 c2 c3 c4"}
 
-    IP, IM, IQ, JP, JM = r("ip"), r("im"), r("iq"), r("jp"), r("jm")
-    LISTS = {"P2": (2, 5), "P3": (0, 2), "P4": (2, 7), "P5": (2, 7)}
-    BANKS = {"P2": 0, "P3": 0, "P4": 4, "P5": 4}
-
-    def pieces(key):
-        ab = [x for bs in calls(key + "a", "G") for x in spans(bs)]
-        return [(a, b, r("ps%d" % (BANKS[key] + k), 0, b - a), "ga%d" % k) for k, (a, b) in enumerate(ab)]
-
-    def chains(key):
-        return [x for bs in calls(key + "v", "C") for x in spans(bs)]
-
-    def orders(key, chain):
+    def words(key):
         names, late = [], []
-        for w in SCHED[key + "v"].split():
+        for w in SCHED[key].split():
             if w[0] == "C":
                 cs = spans([int(v) for v in w.split(":")[1:]])
-                names += ["%s:%d:%d" % (c, a, b) for c in chain for a, b in cs]
+                names += ["%s:%d:%d" % (c, a, b) for c in CHAIN[key[:2]].split() for a, b in cs]
             elif "@" in w:
                 late.append(w.split("@"))
             else:
                 names.append(w)
         for w, i in late:
             names.insert(int(i), w)
-        order("v", names)
-        acts, due = [], []
-        for a, b, ps, ga in pieces(key):
-            acts += ["g:%d:%d" % (a, b)] + due
-            due = [] if "e:%d:%d" % (a, b) in names else ["e:%d:%d" % (a, b)]
-        order("a", acts + due)
+        return names
 
-    def on_vector(key, a, b):
-        return "e:%d:%d" % (a, b) in [w.split("@")[0] for w in SCHED[key + "v"].split()]
+    def calls(key, name):
+        return [tuple(int(v) for v in w.split(":")[1:]) for w in words(key) if w.split(":")[0] == name]
+
+    IP, IM, IQ, JP = r("ip"), r("im"), r("iq"), r("jp")
+    LISTS = {"P2": (2, 5), "P3": (0, 2), "P4": (2, 7), "P5": (2, 7)}
+
+    def pieces(key):
+        return [(a, b, r("ps%d" % (k + (4 if key in ("P4", "P5") else 0)), 0, b - a), "ga%d" % k)
+                for k, (a, b) in enumerate(calls(key + "a", "g"))]
+
+    def readout(key, a, b):
+        return "v" if (a, b) in calls(key + "v", "e") else "a"
 
     xs = spans([S * i // SCHED["xparts"] for i in range(SCHED["xparts"] + 1)])
     load("a", [r("sl", 0, 12)], T.sl[:, 0:12], T.spsend[:])
-    load("a", [r("sl", 12, 24)], T.sl[:, 12:24], T.rxsend[:])
     load("s", [r("ri")], T.ri[0:32, :], T.rate[:])
     for a, b in xs:
-        load("s", [r("xi", a, b)], T.xi[:, a:b], T.x[:, a:b])
+        load("s", [r("n0", O + a, O + b)], T.n0[:, O + a:O + b], T.x[:, a:b])
+    load("s", [r("sl", 12, 24)], T.sl[:, 12:24], T.rxsend[:])
     load("s", [r("li", 0, 256)], T.li[:, 0:2, :], T.reac[:])
     load("s", [r("li", 256, 640)], T.li[:, 2:5, :], T.cons[:])
     load("s", [r("li", 640, 896)], T.li[:, 5:7, :], T.prod[:])
     add("v", "ones", lambda: V.memset(ap(r("ones")), 1.0), [], [r("ones")])
     add("v", "zz0", lambda: V.memset(ap(r("zz")), 0.0), [], [r("zz")])
     for t in range(STEPS):
-        for w, c in (("e", 253.0), ("h", 0.0)):
+        for w, c in (("e", 255.0), ("h", 0.0)):
             add("v", "no", lambda x=r("%s%d" % (w, t), NONE, WW), c=c: V.memset(ap(x), c), [], [r("%s%d" % (w, t), NONE, WW)])
     add("p", "i1", lambda: g.iota(ap(r("it", 0, 16)), [[-1, 16]], 16, 1), [], [r("it", 0, 16)])
     add("p", "i2", lambda: g.iota(ap(r("it", 16, 24)), [[-16, 8]], 0, 1), [], [r("it", 16, 24)])
-    add("p", "ip", lambda: g.affine_select(ap(IP), ap(r("ones", 0, 128)), [[-1, 128]], A.is_equal, 0.0, 0, 1), [r("ones")], [IP])
     add("p", "sel", lambda: g.affine_select(ap(r("sel", parts=32)), ap(r("ones", parts=32)), [[-1, 4], [-4, 8], [0, 16]],
                                             A.is_equal, 0.0, 0, 1), [r("ones")], [r("sel")])
+    add("p", "ip", lambda: g.affine_select(ap(IP), ap(r("ones", 0, 128)), [[-1, 128]], A.is_equal, 0.0, 0, 1), [r("ones")], [IP])
     ts("ian", r("iu", 0, 16), r("it", 0, 16), 15, None, A.bitwise_and)
     ts("iz", r("iu", 16, 24), r("it", 16, 24), 4, None, A.arith_shift_right)
-    ts("im", IM, IP, -1.0, None, A.mult)
     ts("idb", r("idb"), r("iu", 0, 16), 0.0, None, A.is_equal)
     ts("zz1", r("zz", 15, 143, 16), r("iu", 16, 24), 0.0, None, A.is_equal)
-    ts("iq", IQ, IP, -4.0, None, A.mult)
-    act("jp", JP, IP, F.Copy)
-    act("jm", JM, IM, F.Copy)
-    ts("hi", r("hl", 0, 24), r("sl"), 4, None, A.arith_shift_right)
-    ts("lo", r("hl", 24, 48), r("sl"), 15, None, A.bitwise_and)
-    cp("su", r("su"), r("sl"))
-    cp("hu", r("hu"), r("hl"))
     cp("rb", r("rb", parts=32), r("ri", parts=32))
-    act("mk1", r("mk", O, 2 * O), r("idb"), F.Copy, off=r("hu", 36, 48))
-    act("mk0", r("mk", 0, O), r("idb"), F.Copy, off=r("hu", 24, 36))
+
+    def split(s):
+        cp("su", r("su", 12 * s, 12 * s + 12), r("sl", 12 * s, 12 * s + 12))
+        ts("hi", r("hl", 24 * s, 24 * s + 12), r("sl", 12 * s, 12 * s + 12), 4, None, A.arith_shift_right)
+        ts("lo", r("hl", 24 * s + 12, 24 * s + 24), r("sl", 12 * s, 12 * s + 12), 15, None, A.bitwise_and)
+
+    def mask(s):
+        cp("hu", r("hu", 24 * s, 24 * s + 24), r("hl", 24 * s, 24 * s + 24))
+        act("mk", r("mk", O * s, O * s + O), r("idb"), F.Copy, off=r("hu", 24 * s + 12, 24 * s + 24))
 
     def compose(l0, l1, bank):
-        s = 1 if l0 < 2 else 0
+        s, src, xx, zz = (1, "lc", "xx", "zz") if l0 < 2 else (0, "li", "xw", "zw")
         for l in range(l0, l1):
-            tt("X", r("xx", O * l, O * l + O), r("li", 128 * l, 128 * l + 128), r("mk", O * s, O * s + O), A.mult,
-               off=r("hu", 12 * s, 12 * s + 12))
-        mm([(r(bank, 0, 12 * (l1 - l0)), r("zz", 15 - u, 143 - u), r("xx", O * l0 + u, O * l1, 16)) for u in range(16)])
+            tt("X", r(xx, O * (l - l0), O * (l - l0 + 1)), r(src, 128 * l, 128 * l + 128), r("mk", O * s, O * s + O), A.mult,
+               off=r("hu", 24 * s, 24 * s + 12))
+        mm([(r(bank, 0, 12 * (l1 - l0)), r(zz, 15 - u, 143 - u), r(xx, u, O * (l1 - l0), 16)) for u in range(16)])
 
     def narrow(l0, l1, end):
         add("v", "lu", lambda: V.tensor_copy(T.lu[:, l0:l1, 12:end // 16], T.li[:, l0:l1, 0:(end - O) // 16]),
@@ -303,37 +303,54 @@ def rank_program(g, core, T, topo):
         for a, b, ps, ga in pieces(key):
             if a < O:
                 offs[(l0, l1, a, b)] = r("la", 0, 12 * (l1 - l0))
-            elif (l0, l1, a, b) not in offs:
+            elif (l0, 7, a, b) in offs:
+                out = offs[(l0, 7, a, b)]
+                offs[(l0, l1, a, b)] = r("la", out[1], out[1] + (b - a) // 16 * (l1 - l0))
+            else:
                 out = r("la", fill[0], fill[0] + (b - a) // 16 * (l1 - l0))
                 offs[(l0, l1, a, b)] = out
-                fill[0] = out[2]
-                add("v", "la", lambda out=out, a=a, b=b: V.tensor_copy(ap(out), T.li[:, l0:l1, (a - O) // 16:(b - O) // 16]),
+                fill[0] = out[2] + out[2] % 2
+                add("a", "la", lambda out=out, a=a, b=b: SC.activation(ap(out), T.li[:, l0:l1, (a - O) // 16:(b - O) // 16], F.Copy),
                     [r("li", 128 * l0, 128 * l1)], [out])
 
-    for u in (3, 2, 1, 0):
-        mm([(r("ps%d" % (u + 1)), r("sel", 128 * u, 128 * u + 128, parts=32), r("rb", parts=32))])
-        act("kk", r("kk", O + 512 * u, O + 512 * u + 512), r("ps%d" % (u + 1)), F.Copy, scale=-1.25 / 1024)
-    act("kc", r("kk", 0, O), win("kk"), F.Copy, off=r("su", 12, 24))
     kh = min(a for a, b in calls("P1v", "k"))
-    for a, b in xs[:2]:
-        cp("cv", r("n0", O + a, O + b), r("xi", a, b))
-    cp("xc", r("n0", 0, O), r("xi"), off=r("su", 0, 12))
-    exchange("n0")
-    compose(0, 2, "ps0")
-    if SCHED["akh"]:
-        act("kh", r("kh", kh, U), r("kk", kh, U), F.Copy)
-    else:
-        cp("kh", r("kh", kh, U), r("kk", kh, U))
-    for a, b in xs[2:]:
-        if SCHED["acv"]:
-            act("cv", r("n0", O + a, O + b), r("xi", a, b), F.Copy)
+    split(0)
+    act("zw", r("zw"), r("zz"), F.Copy)
+    mask(0)
+    ts("im", IM, IP, -1.0, None, A.mult)
+    ts("iq", IQ, IP, -4.0, None, A.mult)
+
+    def rates(u, q):
+        mm([(r("ps%d" % (4 + u)), r("sel", 128 * u, 128 * u + 128, parts=32), r("rb", parts=32))])
+        if q == "v":
+            ts("kk", r("kk", O + 512 * u, O + 512 * u + 512), r("ps%d" % (4 + u)), KS, None, A.mult)
         else:
-            cp("cv", r("n0", O + a, O + b), r("xi", a, b))
-    compose(2, 7, "ps7")
+            act("kk", r("kk", O + 512 * u, O + 512 * u + 512), r("ps%d" % (4 + u)), F.Copy, scale=KS)
+
+    rates(3, "a")
+    rates(2, "a")
+    cp("xc", r("n0", 0, O), r("n0", O, U), off=r("su", 0, 12))
+    exchange("n0")
+    add("p", "jp", lambda: g.affine_select(ap(JP), ap(r("ones", 0, 128)), [[-1, 128]], A.is_equal, 0.0, 0, 1), [r("ones")], [JP])
+    split(1)
     narrow(0, 2, U)
-    add("v", "cu", lambda: V.tensor_copy(T.lu[:, 0:2, 0:12], T.ps0[:, 0:24]), [r("ps0")], [lst(0, 0, O), lst(1, 0, O)])
-    narrow(2, 7, max(b for key in ("P2", "P4", "P5") for a, b in chains(key)))
-    for key in LISTS:
+    act("lc", r("lc", 0, 256), r("li", 0, 256), F.Identity, -MID, 1.0)
+    mask(1)
+    rates(1, "a")
+    rates(0, SCHED["last rates"])
+    act("kc", r("kk", 0, O), win("kk"), F.Copy, off=r("su", 12, 24))
+    act("kh", r("kh", kh, U), r("kk", kh, U), F.Copy)
+    nb = min(a for key in ("P2", "P4") for a, b, ps, ga in pieces(key) if a >= O)
+    for a, b in ((0, O), (nb, U)):
+        add("p", "nb", lambda a=a, b=b: g.affine_select(ap(r("nb", a, b)), ap(r("n0", a, b)), [[0, b - a]], A.is_equal, 0.0, 0, 0),
+            [r("n0", a, b)], [r("nb", a, b)])
+    piece_lists("P3")
+    narrow(2, 7, max(b for key in ("P2", "P4", "P5") for a, b in calls(key + "v", "c0")))
+    compose(0, 2, "ps0")
+    compose(2, 7, "ps3")
+    add("v", "cu", lambda: V.tensor_scalar(T.lu[:, 0:2, 0:12], T.ps0[:, 0:24], MID, None, A.add), [r("ps0")],
+        [lst(0, 0, O), lst(1, 0, O)])
+    for key in ("P4", "P5", "P2"):
         piece_lists(key)
 
     def part(buf, l, w):
@@ -341,93 +358,87 @@ def rank_program(g, core, T, topo):
 
     stores = [0]
     for t in range(STEPS):
-        n, e, f, m, h = "n%d" % t, "e%d" % t, "f%d" % t, "m%d" % t, "h%d" % t
+        n, e, f, m, h = "n%d" % t, "e%d" % t, "ff", "m%d" % t, "h%d" % t
         last = t == STEPS - 1
         k4 = "P5" if last else "P4"
         phase[0] += 1
-        g2 = [mm([(ps, JM, r(n, a, b))]) for a, b, ps, ga in pieces("P2")]
-        for a, b in calls("P1a", "x"):
-            act("x:%d:%d" % (a, b), r("x1", a, b), win(n), F.Copy, off=lst(0, a, b))
-        for a, b in calls("P1a", "y"):
-            act("y:%d:%d" % (a, b), r("x2", a, b), win(n), F.Copy, off=lst(1, a, b))
-        both = [c for a, b in calls("P1v", "u") for c in range(a, b)]
-        for a, b in calls("P1v", "t"):
-            tt("t:%d:%d" % (a, b), r("tf" if a in both else "kx", a, b), win(n), r("kk", a, b), A.mult, off=lst(1, a, b))
-        for a, b in calls("P1v", "u"):
-            tt("u:%d:%d" % (a, b), r("tf", a, b), win(n), r("tf", a, b), A.mult, off=lst(0, a, b))
-        for a, b in calls("P1v", "k"):
-            times("k:%d:%d" % (a, b), r("kx", a, b), r("x2", a, b), r("kh", a, b))
-        for a, b in calls("P1v", "s"):
-            times("s:%d:%d" % (a, b), r("zh", a, b), r("x1", a, b), r("kx", a, b))
-        for a, b in calls("P1a", "F"):
-            act("F:%d:%d" % (a, b), r(e, a, b), r("tf" if a in both else "zh", a, b), F.Identity, 252.5 + 0.4 / 1024, -0.8)
-        for a, b in calls("P1v", "F"):
-            ts("F:%d:%d" % (a, b), r(e, a, b), r("tf" if a in both else "zh", a, b), -0.8, 252.5 + 0.4 / 1024, A.mult, A.add)
-        exchange(e)
-        names = SCHED["P1v"].split()
-        if t == 0:
-            cp("cu", r("la", 0, 60), r("ps7", 0, 60))
-            names.insert(names.index("F:0:192") + 1, "cu")
-        order("v", names)
-        order("a", SCHED["P1a"].split())
-        phase[0] += 1
-        ts("P", r(f), r(e), 256.0, 253.0, A.min, A.subtract)
-        for a, b in chains("P2"):
-            for l in range(3):
-                tt("c%d:%d:%d" % (l, a, b), r("tb", a, b), win(f), r("tb" if l else n, a, b), A.add if l else A.subtract,
-                   off=lst(2 + l, a, b))
-            ts("M:%d:%d" % (a, b), r(m, a, b), r("tb", a, b), 0.0, 4.0, A.is_le, A.mult)
-        g4 = []
+        sums = {}
 
-        def counts_ahead(upto):
-            for a4, b4, ps4, ga4 in pieces(k4)[len(g4):upto]:
-                g4.append(mm([(ps4, JP, r(n, a4, b4))]))
+        def counts(key, when):
+            for i2, (a2, b2, ps2, ga2) in enumerate(pieces(key)):
+                if SCHED["counts"][key][i2] == when:
+                    sums[(key, i2)] = mm([(ps2, JP if t else IP, r(n if t else "nb", a2, b2))])
+        if t == 0:
+            cp("cu", r("la", 0, 60), r("ps3", 0, 60))
+        counts("P2", 0)
+        counts(k4, 0)
+        for a, b in calls("P1a", "x"):
+            act("P1x:%d:%d" % (a, b), r("x1", a, b), win(n), F.Copy, scale=1.5, off=lst(0, a, b))
+        for a, b in calls("P1a", "y"):
+            act("P1y:%d:%d" % (a, b), r("x2", a, b), win(n), F.Copy, off=lst(1, a, b))
+        for a, b in calls("P1v", "t"):
+            tt("P1t:%d:%d" % (a, b), r("kx", a, b), win(n), r("kk", a, b), A.mult, off=lst(1, a, b))
+        for a, b in calls("P1v", "k"):
+            times("P1k:%d:%d" % (a, b), r("kx", a, b), r("x2", a, b), r("kh", a, b))
+        for a, b in calls("P1v", "s"):
+            times("P1s:%d:%d" % (a, b), r("zh", a, b), r("x1", a, b), r("kx", a, b))
+        for a, b in calls("P1v", "F"):
+            ts("P1F:%d:%d" % (a, b), r(e, a, b), r("zh", a, b), -3.0, 255.5 - 0.4 / 1024, A.max, A.add)
+        exchange(e)
+        for key in ("P1", "P2", "P3"):
+            for a, b in calls(key + "v", "f"):
+                ts("%sf:%d:%d" % (key, a, b), r(f, a, b), r(e, a, b), -1.0, 255.0, A.mult, A.add)
+            for a, b in calls(key + "a", "f"):
+                act("%sf:%d:%d" % (key, a, b), r(f, a, b), r(e, a, b), F.Identity, 255.0, -1.0)
+        for a, b in calls("P2v", "c0"):
+            for l in range(3):
+                tt("P2c%d:%d:%d" % (l, a, b), r("tb", a, b), win(e), r("tb" if l else n, a, b), A.add, off=lst(2 + l, a, b))
+            ts("P2M:%d:%d" % (a, b), r(m, a, b), r("tb", a, b), 765.0, 4.0, A.is_ge, A.mult)
         for i, (a, b, ps, ga) in enumerate(pieces("P2")):
-            act("g:%d:%d" % (a, b), r(ga, 0, 3 * (b - a)), win(e), F.Relu, 256.0, -1.0, off=offs[LISTS["P2"] + (a, b)])
-            mm([(ps, IM, part(ga, l, b - a)) for l in range(3)], g2[i])
-            if on_vector("P2", a, b):
-                ts("e:%d:%d" % (a, b), r(m, a, b), ps, -9.0, 4.0, A.is_le, A.mult)
+            act("P2g:%d:%d" % (a, b), r(ga, 0, 3 * (b - a)), win(e), F.Copy, off=offs[LISTS["P2"] + (a, b)])
+            mm([(ps, IP, part(ga, l, b - a)) for l in range(3)], sums[("P2", i)])
+            counts("P2", 1 + i)
+            counts(k4, 1 + i if i < 3 else -1)
+            if readout("P2", a, b) == "v":
+                ts("P2e:%d:%d" % (a, b), r(m, a, b), ps, 765.0, 4.0, A.is_ge, A.mult)
             else:
-                act("e:%d:%d" % (a, b), r(m, a, b), ps, F.Relu, -32.0, -4.0)
-            counts_ahead(SCHED["ahead"][0][i])
+                act("P2e:%d:%d" % (a, b), r(m, a, b), ps, F.Relu, -4 * 764.0, 4.0)
         exchange(m)
-        orders("P2", ["c0", "c1", "c2", "M"])
-        phase[0] += 1
-        for a, b in chains("P3"):
-            tt("c0:%d:%d" % (a, b), r("tb", a, b), win(m), r(f, a, b), A.min, off=lst(0, a, b))
-            tt("c1:%d:%d" % (a, b), r(h, a, b), win(m), r("tb", a, b), A.min, off=lst(1, a, b))
-        g3 = [mm([(ps, IP, r(f, a, b))]) for a, b, ps, ga in pieces("P3")]
+        for a, b in calls("P3v", "c0"):
+            tt("P3c0:%d:%d" % (a, b), r("tb", a, b), win(m), r(f, a, b), A.min, off=lst(0, a, b))
+            tt("P3c1:%d:%d" % (a, b), r(h, a, b), win(m), r("tb", a, b), A.min, off=lst(1, a, b))
+        g3 = [mm([(ps, IM, r(e, a, b))]) for a, b, ps, ga in pieces("P3")]
         for i, (a, b, ps, ga) in enumerate(pieces("P3")):
-            act("g:%d:%d" % (a, b), r(ga, 0, 2 * (b - a)), win(m), F.Relu, 1.0, -1.0, off=offs[LISTS["P3"] + (a, b)])
+            act("P3g:%d:%d" % (a, b), r(ga, 0, 2 * (b - a)), win(m), F.Relu, 1.0, -1.0, off=offs[LISTS["P3"] + (a, b)])
             mm([(ps, IQ, part(ga, l, b - a)) for l in range(2)], g3[i])
-            if on_vector("P3", a, b):
-                ts("e:%d:%d" % (a, b), r(h, a, b), ps, 0.0, None, A.max)
+            if readout("P3", a, b) == "v":
+                ts("P3e:%d:%d" % (a, b), r(h, a, b), ps, 255.0, 0.0, A.add, A.max)
             else:
-                act("e:%d:%d" % (a, b), r(h, a, b), ps, F.Relu)
-            counts_ahead(SCHED["ahead"][1][i])
+                act("P3e:%d:%d" % (a, b), r(h, a, b), ps, F.Relu, 255.0, 1.0)
+        counts(k4, 4)
         exchange(h)
-        orders("P3", ["c0", "c1"])
-        phase[0] += 1
         new = "yy" if last else "n%d" % (t + 1)
-        for a, b in chains(k4):
+        for a, b in calls(k4 + "v", "c0"):
             for l in range(5):
-                tt("c%d:%d:%d" % (l, a, b), r(new if l == 4 else "tf", a, b), win(h), r(n if l == 0 else "tf", a, b),
+                tt("%sc%d:%d:%d" % (k4, l, a, b), r(new if l == 4 else "tf", a, b), win(h), r(n if l == 0 else "tf", a, b),
                    A.subtract if l in (0, 3) else A.add, off=lst(2 + l, a, b))
         for i, (a, b, ps, ga) in enumerate(pieces(k4)):
-            act("g:%d:%d" % (a, b), r(ga, 0, 5 * (b - a)), win(h), F.Copy, off=offs[LISTS[k4] + (a, b)])
-            mm([(ps, IM if l < 3 else IP, part(ga, l, b - a)) for l in range(5)], g4[i])
-            if on_vector(k4, a, b):
-                cp("e:%d:%d" % (a, b), r(new, a, b), ps)
+            act("%sg:%d:%d" % (k4, a, b), r(ga, 0, 5 * (b - a)), win(h), F.Copy, off=offs[LISTS[k4] + (a, b)])
+            mm([(ps, IM if l < 3 else IP, part(ga, l, b - a)) for l in range(5)], sums[(k4, i)])
+            counts(k4, 5 + i)
+            if readout(k4, a, b) == "v":
+                cp("%se:%d:%d" % (k4, a, b), r(new, a, b), ps)
             else:
-                act("e:%d:%d" % (a, b), r(new, a, b), ps, F.Copy)
+                act("%se:%d:%d" % (k4, a, b), r(new, a, b), ps, F.Copy)
         if not last:
             exchange(new)
-        orders(k4, ["c0", "c1", "c2", "c3", "c4"])
+        for q in "va":
+            names = [key + w for key in ("P1", "P2", "P3", k4) for w in words(key + q)]
+            if t == 0 and q == "v":
+                names.insert(names.index("P1f:0:192"), "cu")
+            order(q, names)
         if last:
-            ys = []
-            for done in ([(bs[0], bs[-1]) for bs in calls("P5v", "C")], [(a, b) for a, b, ps, ga in pieces("P5")]):
-                ys += [((b - done[0][0]) / (done[-1][1] - done[0][0]), a, b) for a, b in done]
-            for i, (share, a, b) in enumerate(sorted(ys)):
+            for i, (a, b) in enumerate(calls("stores", "y")):
                 add("s", "st%d" % i, lambda a=a, b=b: g.sync.dma_start(T.y[:, a - O:b - O], ap(r("yy", a, b))), [r("yy", a, b)], [],
                     kind="d", sem="stored", count=16)
                 stores[0] += 16

from concourse.bass import DstId, RemoteDMATransfer
from concourse.mybir import AluOpType, ActivationFunctionType

S, O, B, STEPS = 2048, 192, 64, 3
U = O + S
NONE = U + O
WW = NONE + 16
L = U // 16
KS = -(1.0 - 1.8e-4) / 1536
MID = 1120.0

SCHED = {
    "engines": (4, 4),
    "xparts": 1,
    "last rates": "v",
    "counts": {"P2": (0, 0, 0, 1), "P4": (0, 4, 5, 0), "P5": (4, 0, 0, 5)},
    "P1v": "t:0:192 t:192:384 s:0:192 t:384:576 F:0:192 t:576:1568 f:0:192 s:192:1152 k:1568:2240 F:192:1152 s:1152:1600 "
           "s:1600:2016 F:1152:1600 s:2016:2240 F:1600:2016 F:2016:2240",
    "P1a": "x:0:192 x:192:1152 y:1568:2240 x:1152:1600 x:1600:2016 x:2016:2240 f:192:640",
    "P2v": "f:640:896 C:192:768:1344 e:0:192@3",
    "P2a": "g:0:192 g:1344:1808 g:1808:2080 g:2080:2240 e:1344:1808 e:1808:2080 e:2080:2240 f:896:1024",
    "P3v": "c0:0:192 f:1024:1280 c1:0:192 C:192:736:1280",
    "P3a": "g:1280:1696 g:1696:2048 g:2048:2240 e:1280:1696 e:1696:2048 e:2048:2240",
    "P4v": "C:192:768:1360 e:0:192@3",
    "P4a": "g:0:192 g:1360:1808 g:1808:2080 g:2080:2240 e:1360:1808 e:1808:2080 e:2080:2240",
    "P5v": "c0:192:608 c0:608:1024 c1:192:608 c1:608:1024 c2:192:608 c2:608:1024 c3:192:608 c0:1024:1296 c4:192:608 "
           "c1:1024:1296 c3:608:1024 c2:1024:1296 c4:608:1024 c3:1024:1296 e:2080:2240 c4:1024:1296",
    "P5a": "g:1360:1808 g:1808:2080 e:1360:1808 g:2080:2240 e:1808:2080 g:1296:1360 e:1296:1360",
    "stores": "y:1360:1808 y:192:608 y:1808:2080 y:608:1024 y:2080:2240 y:1024:1360",
}

SCRATCH = {
    "nb": ("sbuf", [128, U], "bfloat16"),
    "sl": ("sbuf", [128, 24], "int32"),
    "hl": ("sbuf", [128, 48], "int32"),
    "su": ("sbuf", [128, 24], "uint16"),
    "hu": ("sbuf", [128, 48], "uint16"),
    "li": ("sbuf", [128, 7, 128], "int32"),
    "lc": ("sbuf", [128, 2, 128], "float32"),
    "lu": ("sbuf", [128, 7, L], "uint16"),
    "la": ("sbuf", [128, 1280], "uint16"),
    "ri": ("sbuf", [128, 512], "int32"),
    "rb": ("sbuf", [128, 512], "bfloat16"),
    "kk": ("sbuf", [128, U], "float32"),
    "kh": ("sbuf", [128, U], "float16"),
    "ones": ("sbuf", [128, 512], "bfloat16"),
    "ip": ("sbuf", [128, 128], "bfloat16"),
    "im": ("sbuf", [128, 128], "bfloat16"),
    "iq": ("sbuf", [128, 128], "bfloat16"),
    "jp": ("sbuf", [128, 128], "float32"),
    "sel": ("sbuf", [128, 512], "bfloat16"),
    "it": ("sbuf", [128, 32], "int32"),
    "iu": ("sbuf", [128, 32], "int32"),
    "idb": ("sbuf", [128, 16], "bfloat16"),
    "zz": ("sbuf", [128, 144], "bfloat16"),
    "mk": ("sbuf", [128, 2 * O], "bfloat16"),
    "xx": ("sbuf", [128, 2 * O], "float16"),
    "xw": ("sbuf", [128, 5 * O], "float32"),
    "zw": ("sbuf", [128, 144], "float32"),
    "x1": ("sbuf", [128, U], "float16"),
    "x2": ("sbuf", [128, U], "float16"),
    "kx": ("sbuf", [128, U], "float16"),
    "zh": ("sbuf", [128, U], "float16"),
    "tb": ("sbuf", [128, U], "float16"),
    "tf": ("sbuf", [128, U], "float32"),
    "ff": ("sbuf", [128, U], "bfloat16"),
    "yy": ("sbuf", [128, U], "float32"),
}
for _l in range(4):
    SCRATCH["ga%d" % _l] = ("sbuf", [128, 5 * 512], "bfloat16")
for _t in range(STEPS):
    SCRATCH["n%d" % _t] = ("sbuf", [128, NONE], "float32" if _t else "int32")
    SCRATCH["e%d" % _t] = ("sbuf", [128, WW], "bfloat16")
    SCRATCH["m%d" % _t] = ("sbuf", [128, NONE], "bfloat16")
    SCRATCH["h%d" % _t] = ("sbuf", [128, WW], "bfloat16")
for _b in range(8):
    SCRATCH["ps%d" % _b] = ("psum", [128, 512], "float32")

SEMAPHORES = (["cv", "ca", "ct", "cp", "sent", "stored"] + ["ld%d" % _k for _k in range(12)]
              + ["ar%d" % _k for _k in range(4 * STEPS)])


def rank_program(g, core, T, topo):
    rank = T.rank_of(core)
    if rank is None:
        return
    A, F = AluOpType, ActivationFunctionType
    cores = list(T.cores)
    N = len(cores)
    eng = {"v": g.vector, "a": g.scalar, "t": g.tensor, "p": g, "s": g.sync}
    ops, acc, named = [], {}, {}
    phase = [0]

    def r(name, c0=None, c1=None, step=1, parts=128):
        if c0 is None:
            c0, c1 = 0, SCRATCH[name][1][1]
        return (name, c0, c1, step, parts)

    def ap(x):
        name, c0, c1, step, parts = x
        if len(SCRATCH[name][1]) == 3:
            w = SCRATCH[name][1][2]
            if c1 - c0 > w:
                return T[name][:, c0 // w:c1 // w, :]
            return T[name][:, c0 // w, c0 % w:c0 % w + c1 - c0]
        rows = slice(0, parts) if parts < 128 else slice(None)
        return T[name][rows, c0:c1:step] if step > 1 else T[name][rows, c0:c1]

    def ind(win, off):
        return ap(win).indirect(ap(off))

    def add(q, name, emit, reads, writes, kind="c", sem=None, count=1, group=None):
        k = len(ops)
        deps = set()
        for xs, wr in ((reads, False), (writes, True)):
            for x in xs:
                psum = SCRATCH[x[0]][0] == "psum"
                for (c0, c1, j, w) in acc.get(x[0], []):
                    o = ops[j]
                    if psum:
                        if group is not None and o["group"] == group:
                            continue
                        if w or wr or o["q"] != q:
                            deps.add(j)
                    elif (w or wr) and c0 < x[2] and x[1] < c1:
                        deps.add(j)
        for xs, wr in ((reads, False), (writes, True)):
            for x in xs:
                acc.setdefault(x[0], []).append((x[1], x[2], k, wr))
        ops.append({"q": q, "name": name, "emit": emit, "deps": deps, "kind": kind, "sem": sem, "count": count,
                    "group": group, "phase": phase[0], "pos": k})
        named[(phase[0], q, name)] = k
        return ops[k]

    def order(q, names):
        for i, name in enumerate(names):
            ops[named[(phase[0], q, name)]]["pos"] = i - 10000

    V, SC, PE = g.vector, g.scalar, g.tensor

    def tt(name, out, in0, in1, op, off=None):
        add("v", name, lambda: V.tensor_tensor(ap(out), ind(in0, off) if off else ap(in0), ap(in1), op),
            [in0, in1] + ([off] if off else []), [out])

    def ts(name, out, in0, s1, s2, op0, op1=None):
        def emit():
            if op1 is None:
                return V.tensor_scalar(ap(out), ap(in0), s1, None, op0)
            return V.tensor_scalar(ap(out), ap(in0), s1, s2, op0, op1)
        add("v", name, emit, [in0], [out])

    def times(name, out, in0, in1):
        add("v", name, lambda: V.tensor_tensor_scan(ap(out), ap(in0), ap(in1), 0.0, A.max, A.mult), [in0, in1], [out])

    def cp(name, out, in_, off=None):
        add("v", name, lambda: V.tensor_copy(ap(out), ind(in_, off) if off else ap(in_)), [in_] + ([off] if off else []), [out])

    def act(name, out, in_, func, bias=None, scale=None, off=None):
        def emit():
            src = ind(in_, off) if off else ap(in_)
            if scale is None:
                return SC.activation(ap(out), src, func)
            if bias is None:
                return SC.activation(ap(out), src, func, scale=scale)
            return SC.activation(ap(out), src, func, bias=bias, scale=scale)
        add("a", name, emit, [in_] + ([off] if off else []), [out])

    groups, members, opened = [0], {}, {}

    def mm(terms, group=None):
        if group is None:
            groups[0] += 1
            group = groups[0]
        for (out, lhs, rhs) in terms:
            add("t", "mm%d" % len(ops), lambda out=out, lhs=lhs, rhs=rhs: (ap(out), ap(lhs), ap(rhs)), [lhs, rhs], [out], group=group)
        return group

    loads = [0]

    def load(q, outs, dst, src):
        sem = "ld%d" % loads[0]
        loads[0] += 1
        add(q, sem, lambda: eng[q].dma_start(dst, src), [], outs, kind="d", sem=sem, count=16)

    peers = [cores[(rank + 1 + m) % N] for m in range(N - 1)]

    def masks_of(src):
        used, res = [], {}
        for d in sorted([c for c in cores if c != src], key=lambda d: len(topo.engines(src, d))):
            want = SCHED["engines"][1 if topo.chip(src) == topo.chip(d) else 0]
            e = [x for x in topo.engines(src, d) if x not in used][:want]
            used += e
            res[d] = e
        return res

    mine = masks_of(core)
    arrive = sum(len(masks_of(c)[core]) for c in peers)
    leave = sum(len(e) for e in mine.values())
    sends = [0]

    def exchange(buf):
        sem = "ar%d" % sends[0]
        sends[0] += 1

        def emit():
            trs = []
            for m, d in sorted(enumerate(peers), key=lambda md: topo.chip(md[1]) == topo.chip(core)):
                rid, pid = topo.addr(d)[:2]
                c = U + (N - 2 - m) * B
                trs.append(RemoteDMATransfer(dst_ids=[DstId(rid=rid, pnc=pid)], dma_engine_mask=sum(1 << e for e in mine[d]),
                                             remote_sem=T.sem[sem], src=T[buf][:, m * B:(m + 1) * B], dst=T[buf][:, c:c + B]))
            return g.remote_dma_fused(trs, local_sem=T.sem.sent)
        add("p", "send", emit, [r(buf, 0, O)], [], kind="r")
        add("x", "arrive", None, [], [r(buf, U, NONE)], kind="x", sem=sem, count=arrive)

    def win(buf):
        return r(buf, O, SCRATCH[buf][1][1])

    def lst(l, a, b):
        return r("lu", L * l + a // 16, L * l + b // 16)

    def spans(bs):
        return [(bs[k], bs[k + 1]) for k in range(len(bs) - 1) if bs[k] < bs[k + 1]]

    CHAIN = {"P2": "c0 c1 c2 M", "P3": "c0 c1", "P4": "c0 c1 c2 c3 c4", "P5": "c0 c1 c2 c3 c4"}

    def words(key):
        names, late = [], []
        for w in SCHED[key].split():
            if w[0] == "C":
                cs = spans([int(v) for v in w.split(":")[1:]])
                names += ["%s:%d:%d" % (c, a, b) for c in CHAIN[key[:2]].split() for a, b in cs]
            elif "@" in w:
                late.append(w.split("@"))
            else:
                names.append(w)
        for w, i in late:
            names.insert(int(i), w)
        return names

    def calls(key, name):
        return [tuple(int(v) for v in w.split(":")[1:]) for w in words(key) if w.split(":")[0] == name]

    IP, IM, IQ, JP = r("ip"), r("im"), r("iq"), r("jp")
    LISTS = {"P2": (2, 5), "P3": (0, 2), "P4": (2, 7), "P5": (2, 7)}

    def pieces(key):
        return [(a, b, r("ps%d" % (k + (4 if key in ("P4", "P5") else 0)), 0, b - a), "ga%d" % k)
                for k, (a, b) in enumerate(calls(key + "a", "g"))]

    def readout(key, a, b):
        return "v" if (a, b) in calls(key + "v", "e") else "a"

    xs = spans([S * i // SCHED["xparts"] for i in range(SCHED["xparts"] + 1)])
    load("a", [r("sl", 0, 12)], T.sl[:, 0:12], T.spsend[:])
    load("s", [r("ri")], T.ri[0:32, :], T.rate[:])
    for a, b in xs:
        load("s", [r("n0", O + a, O + b)], T.n0[:, O + a:O + b], T.x[:, a:b])
    load("s", [r("sl", 12, 24)], T.sl[:, 12:24], T.rxsend[:])
    load("s", [r("li", 0, 256)], T.li[:, 0:2, :], T.reac[:])
    load("s", [r("li", 256, 640)], T.li[:, 2:5, :], T.cons[:])
    load("s", [r("li", 640, 896)], T.li[:, 5:7, :], T.prod[:])
    add("v", "ones", lambda: V.memset(ap(r("ones")), 1.0), [], [r("ones")])
    add("v", "zz0", lambda: V.memset(ap(r("zz")), 0.0), [], [r("zz")])
    for t in range(STEPS):
        for w, c in (("e", 255.0), ("h", 0.0)):
            add("v", "no", lambda x=r("%s%d" % (w, t), NONE, WW), c=c: V.memset(ap(x), c), [], [r("%s%d" % (w, t), NONE, WW)])
    add("p", "i1", lambda: g.iota(ap(r("it", 0, 16)), [[-1, 16]], 16, 1), [], [r("it", 0, 16)])
    add("p", "i2", lambda: g.iota(ap(r("it", 16, 24)), [[-16, 8]], 0, 1), [], [r("it", 16, 24)])
    add("p", "sel", lambda: g.affine_select(ap(r("sel", parts=32)), ap(r("ones", parts=32)), [[-1, 4], [-4, 8], [0, 16]],
                                            A.is_equal, 0.0, 0, 1), [r("ones")], [r("sel")])
    add("p", "ip", lambda: g.affine_select(ap(IP), ap(r("ones", 0, 128)), [[-1, 128]], A.is_equal, 0.0, 0, 1), [r("ones")], [IP])
    ts("ian", r("iu", 0, 16), r("it", 0, 16), 15, None, A.bitwise_and)
    ts("iz", r("iu", 16, 24), r("it", 16, 24), 4, None, A.arith_shift_right)
    ts("idb", r("idb"), r("iu", 0, 16), 0.0, None, A.is_equal)
    ts("zz1", r("zz", 15, 143, 16), r("iu", 16, 24), 0.0, None, A.is_equal)
    cp("rb", r("rb", parts=32), r("ri", parts=32))

    def split(s):
        cp("su", r("su", 12 * s, 12 * s + 12), r("sl", 12 * s, 12 * s + 12))
        ts("hi", r("hl", 24 * s, 24 * s + 12), r("sl", 12 * s, 12 * s + 12), 4, None, A.arith_shift_right)
        ts("lo", r("hl", 24 * s + 12, 24 * s + 24), r("sl", 12 * s, 12 * s + 12), 15, None, A.bitwise_and)

    def mask(s):
        cp("hu", r("hu", 24 * s, 24 * s + 24), r("hl", 24 * s, 24 * s + 24))
        act("mk", r("mk", O * s, O * s + O), r("idb"), F.Copy, off=r("hu", 24 * s + 12, 24 * s + 24))

    def compose(l0, l1, bank):
        s, src, xx, zz = (1, "lc", "xx", "zz") if l0 < 2 else (0, "li", "xw", "zw")
        for l in range(l0, l1):
            tt("X", r(xx, O * (l - l0), O * (l - l0 + 1)), r(src, 128 * l, 128 * l + 128), r("mk", O * s, O * s + O), A.mult,
               off=r("hu", 24 * s, 24 * s + 12))
        mm([(r(bank, 0, 12 * (l1 - l0)), r(zz, 15 - u, 143 - u), r(xx, u, O * (l1 - l0), 16)) for u in range(16)])

    def narrow(l0, l1, end):
        add("v", "lu", lambda: V.tensor_copy(T.lu[:, l0:l1, 12:end // 16], T.li[:, l0:l1, 0:(end - O) // 16]),
            [r("li", 128 * l0, 128 * l1)], [lst(l, O, end) for l in range(l0, l1)])

    offs, fill = {}, [60]

    def piece_lists(key):
        l0, l1 = LISTS[key]
        for a, b, ps, ga in pieces(key):
            if a < O:
                offs[(l0, l1, a, b)] = r("la", 0, 12 * (l1 - l0))
            elif (l0, 7, a, b) in offs:
                out = offs[(l0, 7, a, b)]
                offs[(l0, l1, a, b)] = r("la", out[1], out[1] + (b - a) // 16 * (l1 - l0))
            else:
                out = r("la", fill[0], fill[0] + (b - a) // 16 * (l1 - l0))
                offs[(l0, l1, a, b)] = out
                fill[0] = out[2] + out[2] % 2
                add("a", "la", lambda out=out, a=a, b=b: SC.activation(ap(out), T.li[:, l0:l1, (a - O) // 16:(b - O) // 16], F.Copy),
                    [r("li", 128 * l0, 128 * l1)], [out])

    kh = min(a for a, b in calls("P1v", "k"))
    split(0)
    act("zw", r("zw"), r("zz"), F.Copy)
    mask(0)
    ts("im", IM, IP, -1.0, None, A.mult)
    ts("iq", IQ, IP, -4.0, None, A.mult)

    def rates(u, q):
        mm([(r("ps%d" % (4 + u)), r("sel", 128 * u, 128 * u + 128, parts=32), r("rb", parts=32))])
        if q == "v":
            ts("kk", r("kk", O + 512 * u, O + 512 * u + 512), r("ps%d" % (4 + u)), KS, None, A.mult)
        else:
            act("kk", r("kk", O + 512 * u, O + 512 * u + 512), r("ps%d" % (4 + u)), F.Copy, scale=KS)

    rates(3, "a")
    rates(2, "a")
    cp("xc", r("n0", 0, O), r("n0", O, U), off=r("su", 0, 12))
    exchange("n0")
    add("p", "jp", lambda: g.affine_select(ap(JP), ap(r("ones", 0, 128)), [[-1, 128]], A.is_equal, 0.0, 0, 1), [r("ones")], [JP])
    split(1)
    narrow(0, 2, U)
    act("lc", r("lc", 0, 256), r("li", 0, 256), F.Identity, -MID, 1.0)
    mask(1)
    rates(1, "a")
    rates(0, SCHED["last rates"])
    act("kc", r("kk", 0, O), win("kk"), F.Copy, off=r("su", 12, 24))
    act("kh", r("kh", kh, U), r("kk", kh, U), F.Copy)
    nb = min(a for key in ("P2", "P4") for a, b, ps, ga in pieces(key) if a >= O)
    for a, b in ((0, O), (nb, U)):
        add("p", "nb", lambda a=a, b=b: g.affine_select(ap(r("nb", a, b)), ap(r("n0", a, b)), [[0, b - a]], A.is_equal, 0.0, 0, 0),
            [r("n0", a, b)], [r("nb", a, b)])
    piece_lists("P3")
    narrow(2, 7, max(b for key in ("P2", "P4", "P5") for a, b in calls(key + "v", "c0")))
    compose(0, 2, "ps0")
    compose(2, 7, "ps3")
    add("v", "cu", lambda: V.tensor_scalar(T.lu[:, 0:2, 0:12], T.ps0[:, 0:24], MID, None, A.add), [r("ps0")],
        [lst(0, 0, O), lst(1, 0, O)])
    for key in ("P4", "P5", "P2"):
        piece_lists(key)

    def part(buf, l, w):
        return r(buf, l * w, l * w + w)

    stores = [0]
    for t in range(STEPS):
        n, e, f, m, h = "n%d" % t, "e%d" % t, "ff", "m%d" % t, "h%d" % t
        last = t == STEPS - 1
        k4 = "P5" if last else "P4"
        phase[0] += 1
        sums = {}

        def counts(key, when):
            for i2, (a2, b2, ps2, ga2) in enumerate(pieces(key)):
                if SCHED["counts"][key][i2] == when:
                    sums[(key, i2)] = mm([(ps2, JP if t else IP, r(n if t else "nb", a2, b2))])
        if t == 0:
            cp("cu", r("la", 0, 60), r("ps3", 0, 60))
        counts("P2", 0)
        counts(k4, 0)
        for a, b in calls("P1a", "x"):
            act("P1x:%d:%d" % (a, b), r("x1", a, b), win(n), F.Copy, scale=1.5, off=lst(0, a, b))
        for a, b in calls("P1a", "y"):
            act("P1y:%d:%d" % (a, b), r("x2", a, b), win(n), F.Copy, off=lst(1, a, b))
        for a, b in calls("P1v", "t"):
            tt("P1t:%d:%d" % (a, b), r("kx", a, b), win(n), r("kk", a, b), A.mult, off=lst(1, a, b))
        for a, b in calls("P1v", "k"):
            times("P1k:%d:%d" % (a, b), r("kx", a, b), r("x2", a, b), r("kh", a, b))
        for a, b in calls("P1v", "s"):
            times("P1s:%d:%d" % (a, b), r("zh", a, b), r("x1", a, b), r("kx", a, b))
        for a, b in calls("P1v", "F"):
            ts("P1F:%d:%d" % (a, b), r(e, a, b), r("zh", a, b), -3.0, 255.5 - 0.4 / 1024, A.max, A.add)
        exchange(e)
        for key in ("P1", "P2", "P3"):
            for a, b in calls(key + "v", "f"):
                ts("%sf:%d:%d" % (key, a, b), r(f, a, b), r(e, a, b), -1.0, 255.0, A.mult, A.add)
            for a, b in calls(key + "a", "f"):
                act("%sf:%d:%d" % (key, a, b), r(f, a, b), r(e, a, b), F.Identity, 255.0, -1.0)
        for a, b in calls("P2v", "c0"):
            for l in range(3):
                tt("P2c%d:%d:%d" % (l, a, b), r("tb", a, b), win(e), r("tb" if l else n, a, b), A.add, off=lst(2 + l, a, b))
            ts("P2M:%d:%d" % (a, b), r(m, a, b), r("tb", a, b), 765.0, 4.0, A.is_ge, A.mult)
        for i, (a, b, ps, ga) in enumerate(pieces("P2")):
            act("P2g:%d:%d" % (a, b), r(ga, 0, 3 * (b - a)), win(e), F.Copy, off=offs[LISTS["P2"] + (a, b)])
            mm([(ps, IP, part(ga, l, b - a)) for l in range(3)], sums[("P2", i)])
            counts("P2", 1 + i)
            counts(k4, 1 + i if i < 3 else -1)
            if readout("P2", a, b) == "v":
                ts("P2e:%d:%d" % (a, b), r(m, a, b), ps, 765.0, 4.0, A.is_ge, A.mult)
            else:
                act("P2e:%d:%d" % (a, b), r(m, a, b), ps, F.Relu, -4 * 764.0, 4.0)
        exchange(m)
        for a, b in calls("P3v", "c0"):
            tt("P3c0:%d:%d" % (a, b), r("tb", a, b), win(m), r(f, a, b), A.min, off=lst(0, a, b))
            tt("P3c1:%d:%d" % (a, b), r(h, a, b), win(m), r("tb", a, b), A.min, off=lst(1, a, b))
        g3 = [mm([(ps, IM, r(e, a, b))]) for a, b, ps, ga in pieces("P3")]
        for i, (a, b, ps, ga) in enumerate(pieces("P3")):
            act("P3g:%d:%d" % (a, b), r(ga, 0, 2 * (b - a)), win(m), F.Relu, 1.0, -1.0, off=offs[LISTS["P3"] + (a, b)])
            mm([(ps, IQ, part(ga, l, b - a)) for l in range(2)], g3[i])
            if readout("P3", a, b) == "v":
                ts("P3e:%d:%d" % (a, b), r(h, a, b), ps, 255.0, 0.0, A.add, A.max)
            else:
                act("P3e:%d:%d" % (a, b), r(h, a, b), ps, F.Relu, 255.0, 1.0)
        counts(k4, 4)
        exchange(h)
        new = "yy" if last else "n%d" % (t + 1)
        for a, b in calls(k4 + "v", "c0"):
            for l in range(5):
                tt("%sc%d:%d:%d" % (k4, l, a, b), r(new if l == 4 else "tf", a, b), win(h), r(n if l == 0 else "tf", a, b),
                   A.subtract if l in (0, 3) else A.add, off=lst(2 + l, a, b))
        for i, (a, b, ps, ga) in enumerate(pieces(k4)):
            act("%sg:%d:%d" % (k4, a, b), r(ga, 0, 5 * (b - a)), win(h), F.Copy, off=offs[LISTS[k4] + (a, b)])
            mm([(ps, IM if l < 3 else IP, part(ga, l, b - a)) for l in range(5)], sums[(k4, i)])
            counts(k4, 5 + i)
            if readout(k4, a, b) == "v":
                cp("%se:%d:%d" % (k4, a, b), r(new, a, b), ps)
            else:
                act("%se:%d:%d" % (k4, a, b), r(new, a, b), ps, F.Copy)
        if not last:
            exchange(new)
        for q in "va":
            names = [key + w for key in ("P1", "P2", "P3", k4) for w in words(key + q)]
            if t == 0 and q == "v":
                names.insert(names.index("P1f:0:192"), "cu")
            order(q, names)
        if last:
            for i, (a, b) in enumerate(calls("stores", "y")):
                add("s", "st%d" % i, lambda a=a, b=b: g.sync.dma_start(T.y[:, a - O:b - O], ap(r("yy", a, b))), [r("yy", a, b)], [],
                    kind="d", sem="stored", count=16)
                stores[0] += 16

    queue = {}
    for k, o in enumerate(ops):
        queue.setdefault(o["q"], []).append(k)
        members[o["group"]] = members.get(o["group"], 0) + 1
    for q in queue:
        queue[q].sort(key=lambda k: (ops[k]["phase"], ops[k]["pos"]))
    head = dict((q, 0) for q in queue)
    seq, place = [], {}
    while len(seq) < len(ops):
        cand = [queue[q][head[q]] for q in queue if head[q] < len(queue[q])]
        cand = [k for k in cand if all(d in place for d in ops[k]["deps"])]
        assert cand, "the queues' orders contradict the data's order"
        k = min(cand)
        head[ops[k]["q"]] += 1
        place[k] = len(seq)
        seq.append(k)

    count = dict((q, 0) for q in "vatp")
    known = dict((q, {}) for q in "vatps")
    clock, token, waited = {}, {}, {}
    for k in seq:
        o = ops[k]
        q = o["q"]
        if o["kind"] == "x":
            token[k] = (o["sem"], o["count"])
            clock[k] = {o["sem"]: o["count"]}
            continue
        kn = known[q]
        for d in sorted(o["deps"], key=lambda d: -place[d]):
            sem, val = token[d]
            if kn.get(sem, 0) >= val:
                continue
            eng[q].wait_ge(T.sem[sem], val)
            waited[sem] = max(waited.get(sem, 0), val)
            for s2, v2 in clock[d].items():
                if kn.get(s2, 0) < v2:
                    kn[s2] = v2
        ins = o["emit"]()
        if q == "t":
            opened[o["group"]] = opened.get(o["group"], 0) + 1
            ins = PE.matmul(ins[0], ins[1], ins[2], opened[o["group"]] == 1, opened[o["group"]] == members[o["group"]])
        if o["kind"] == "c":
            count[q] += 1
            token[k] = ("c" + q, count[q])
            ins.then_inc(T.sem["c" + q], 1)
        elif o["kind"] == "d":
            token[k] = (o["sem"], o["count"])
            ins.then_inc(T.sem[o["sem"]], 16)
        if o["kind"] != "r":
            clock[k] = dict(kn)
            clock[k][token[k][0]] = token[k][1]
    for q in "vatp":
        if waited.get("c" + q, 0) < count[q]:
            g.wait_ge(T.sem["c" + q], count[q])
    g.wait_ge(T.sem.sent, leave * sends[0])
    g.sync.wait_ge(T.sem.stored, stores[0])
